import numpy as np
import ml_dtypes


def mxq(x, axis, fmt="e4m3"):
    dtype, down = {"e4m3": (ml_dtypes.float8_e4m3fn, 7), "e5m2": (ml_dtypes.float8_e5m2, 14)}[fmt]
    v = np.moveaxis(np.asarray(x, np.float32).astype(ml_dtypes.bfloat16).astype(np.float64), axis, -1)
    blocks = v.reshape(v.shape[:-1] + (-1, 32))
    amax = np.abs(blocks).max(-1, keepdims=True)
    byte = np.maximum(np.where(amax > 0, np.frexp(amax)[1] - 1 + 127, 0) - down, 1)
    scale = np.exp2(byte - 127.0)
    codes = (blocks / scale).astype(np.float32).astype(dtype).astype(np.float64)
    return np.moveaxis((codes * scale).reshape(v.shape), -1, axis)


WIDE = False


def mx_kscale(k):
    if not WIDE:
        return np.ones(k)
    levels = np.array([10, -10, 5, -5, 0])
    if k % 512:
        return np.exp2(np.random.permutation(np.resize(levels, k // 32))).repeat(32)
    a = np.empty((k // 512, 16))
    for p in range(k // 512):
        a[p, :8] = np.random.permutation(np.resize(levels, 8))
        for g in range(8):
            far = levels[np.abs(levels - a[p, g]) >= 10]
            a[p, g + 8] = far[np.random.randint(len(far))]
    return np.exp2(a.ravel()).repeat(32)


def f64(x):
    return np.asarray(x).astype(np.float64)


def striped(idx):
    return np.tile(idx.reshape(-1, 16).T, (8, 1)).astype(np.uint16)


def unstriped(offs):
    return offs[:16].T.reshape(-1).astype(np.int64)


E2M1 = np.array([0.0, 0.5, 1.0, 1.5, 2.0, 3.0, 4.0, 6.0, -0.0, -0.5, -1.0, -1.5, -2.0, -3.0, -4.0, -6.0])


def pack_weight(w, fmt):
    k, n = w.shape
    w = f64(np.asarray(w, np.float32).astype(ml_dtypes.bfloat16)).reshape(k // 32, 32, n)
    amax = np.abs(w).max(1)
    if fmt == "e4m3":
        byte = np.frexp(amax)[1] - 1 + 127 - 7
    else:
        mant, ex = np.frexp(amax / 6.0)
        byte = np.where(mant > 0.5, ex, ex - 1) + 127
    byte = np.clip(np.where(amax > 0, byte, 1), 1, 254)
    scaled = (w * np.exp2(127.0 - byte)[:, None, :]).reshape(k, n).astype(np.float32)
    by_word = np.ascontiguousarray(scaled.reshape(k // 512, 128, 4, n).transpose(0, 1, 3, 2))
    if fmt == "e4m3":
        words = by_word.astype(ml_dtypes.float8_e4m3fn).view(np.uint8)
    else:
        c = by_word.astype(ml_dtypes.float4_e2m1fn).view(np.uint8) & 0xF
        words = (c[..., 0::2] | (c[..., 1::2] << 4)).reshape(k // 512, 128, 2 * n)
    return np.ascontiguousarray(words), np.ascontiguousarray(byte.astype(np.uint8).reshape(k // 512, 16, n))


def unpack_weight(words, scales, fmt):
    g, _, n = scales.shape
    words = np.ascontiguousarray(words).reshape(g, 128, n, -1)
    if fmt == "e4m3":
        vals = words.view(ml_dtypes.float8_e4m3fn).astype(np.float64)
    else:
        nib = np.empty((g, 128, n, 4), np.uint8)
        nib[..., 0::2] = words & 0xF
        nib[..., 1::2] = words >> 4
        vals = E2M1[nib]
    vals = vals * np.repeat(np.exp2(scales.astype(np.float64) - 127.0), 8, axis=1)[..., None]
    return vals.transpose(0, 1, 3, 2).reshape(g * 512, n)


def relu2(v):
    return np.maximum(v, 0.0) ** 2


K, T, E, C, N = 1024, 1280, 16, 128, 128
PAD = 32
K8 = 512


def by_expert(wq, xq):
    return np.concatenate([wq[e].T @ xq[:, e * C:(e + 1) * C] for e in range(E)], axis=1)


def setup_inputs():
    n = np.random.standard_normal
    s = mx_kscale(K)[:, None]
    first = np.random.permutation(np.repeat(np.arange(E), T // E))
    second = (first + 1 + np.random.permutation(np.repeat(np.arange(E - 1), -(-T // (E - 1)))[:T])) % E
    while np.bincount(second, minlength=E).max() != T // E:
        load = np.bincount(second, minlength=E); hi, lo = int(load.argmax()), int(load.argmin())
        t = np.flatnonzero((second == hi) & (first != lo))[0]; second[t] = lo
    slot_token = np.empty(E * C, np.int64); pos = np.empty((2, T), np.int64); fill = np.zeros(E, np.int64)
    place = np.stack([np.random.permutation(C) for _ in range(E)])
    for r, deal in enumerate((first, second)):
        for t in np.random.permutation(T):
            e = deal[t]
            if fill[e] < C: j = e * C + place[e, fill[e]]; fill[e] += 1; slot_token[j] = t; pos[r, t] = j
            else: pos[r, t] = E * C + t % PAD
    g = np.random.uniform(0.2, 0.8, T)
    w = n((E, K, N)) / np.sqrt(K) / s[None]
    w8 = [pack_weight(m[:K8], "e4m3") for m in w]
    w4 = [pack_weight(m[K8:], "e2m1") for m in w]
    return {
        "xT": (n((K, T)) * s).astype(np.float32),
        "w8_words": np.stack([m[0] for m in w8]),
        "w8_scales": np.stack([m[1] for m in w8]),
        "w4_words": np.stack([m[0] for m in w4]),
        "w4_scales": np.stack([m[1] for m in w4]),
        "b": (0.3 * n((N, E))).astype(np.float32),
        "gate": np.stack([np.tile(g, (N, 1)), np.tile(1.0 - g, (N, 1))]).astype(np.float32),
        "offs": striped(slot_token),
        "pos1": striped(pos[0]),
        "pos2": striped(pos[1]),
    }


def reference(xT, w8_words, w8_scales, w4_words, w4_scales, b, gate, offs, pos1, pos2):
    idx = unstriped(offs)
    w = np.stack([np.concatenate([unpack_weight(w8_words[e], w8_scales[e], "e4m3"), unpack_weight(w4_words[e], w4_scales[e], "e2m1")]) for e in range(E)])
    xq = mxq(f64(xT)[:, idx], 0, "e4m3")
    y = by_expert(w, xq)
    y = relu2(y + np.repeat(f64(b), C, axis=1))
    y = np.concatenate([y, np.zeros((N, PAD))], axis=1)
    return f64(gate[0]) * y[:, unstriped(pos1)] + f64(gate[1]) * y[:, unstriped(pos2)]

@@ -1,0 +1,211 @@
+from contextlib import ExitStack
+
+import concourse.mybir as mybir
+
+P = 128
+TOKENS = 1280
+EXPERTS = 16
+CAP = 128
+SLOTS = EXPERTS * CAP
+N = 128
+PAD = 32
+K_PASS = 512
+FLOPS = 2 * SLOTS * 2 * K_PASS * N
+
+F32 = mybir.dt.float32
+BF16 = mybir.dt.bfloat16
+U32 = mybir.dt.uint32
+I32 = mybir.dt.int32
+U16 = mybir.dt.uint16
+U8 = mybir.dt.uint8
+FP8X4 = mybir.dt.float8_e4m3fn_x4
+FP4X4 = mybir.dt.float4_e2m1fn_x4
+MULT = mybir.AluOpType.mult
+ADD = mybir.AluOpType.add
+MAX = mybir.AluOpType.max
+RELU = mybir.ActivationFunctionType.Relu
+SQUARE = mybir.ActivationFunctionType.Square
+
+UNIT = 256
+X_LOADS = ((0, 512), (512, 1024), (1024, 1280))
+VECTOR_COLS = (
+    ((256, 512), (768, 1024), (1024, 1184)),
+    ((768, 1024), (1024, 1184)),
+)
+SCALAR_COLS = (
+    ((0, 256), (512, 768), (1184, 1280)),
+    ((0, 256), (256, 512), (512, 768), (1184, 1280)),
+)
+ROW0 = (4, 0)
+GROUPS = ((0, 2), (2, 6), (6, 10), (10, 12), (12, 13), (13, 14), (14, 15), (15, 16))
+ON_VECTOR = 13
+
+
+def tile_moe_cap2_lin_relu2_kernel(
+    tc, xT, w8_words, w8_scales, w4_words, w4_scales, b, gate, offs, pos1, pos2, out
+):
+    nc = tc.nc
+    with ExitStack() as ctx:
+        keep = ctx.enter_context(tc.tile_pool(name="keep", bufs=1))
+        psum = ctx.enter_context(tc.psum_pool(name="psum", bufs=1))
+
+        offs_t = keep.tile([P, SLOTS // 16], U16, name="offs_t")
+        pos1_t = keep.tile([P, TOKENS // 16], U16, name="pos1_t")
+        pos2_t = keep.tile([P, TOKENS // 16], U16, name="pos2_t")
+        bias_t = keep.tile([P, EXPERTS], F32, name="bias_t")
+        gate_t = [keep.tile([P, TOKENS], F32, name=f"gate{c}") for c in range(2)]
+        w8_t = keep.tile([P, EXPERTS * 4 * N], U8, name="w8_t", align_bytes=64)
+        w4_t = keep.tile([P, EXPERTS * 2 * N], U8, name="w4_t", align_bytes=64)
+        ws_t = keep.tile([P, EXPERTS * N], U8, name="ws_t", align_bytes=64)
+        codes = [keep.tile([P, TOKENS], U32, name=f"codes{a}", align_bytes=64) for a in range(2)]
+        scales = keep.tile([P, TOKENS], U8, name="scales", align_bytes=64)
+        slot_codes = [keep.tile([P, SLOTS], U32, name=f"slot_codes{a}", align_bytes=64) for a in range(2)]
+        slot_scales = keep.tile([P, SLOTS], U8, name="slot_scales", align_bytes=64)
+        y = keep.tile([P, SLOTS + PAD], F32, name="y")
+
+        nc.vector.memset(ws_t[:].bitcast(I32), 0)
+        nc.gpsimd.memset(scales[:], 0)
+        ws_i32 = ws_t[:].bitcast(I32).rearrange("p (e n) -> p e n", e=EXPERTS)
+
+        def load_scale_rows(queue, row0, src):
+            rows = src.rearrange("e a q n -> q (e a) n").bitcast(I32)
+            for quad in range(4):
+                queue.dma_start(ws_i32[32 * quad + row0 : 32 * quad + row0 + 4], rows[4 * quad : 4 * quad + 4])
+
+        load_scale_rows(nc.gpsimd, ROW0[0], w8_scales)
+        nc.gpsimd.memset(y[:, SLOTS:], 0.0)
+
+        x_raw = [
+            {lo: keep.tile([P, 4, hi - lo], F32, name=f"raw{a}_{lo}") for lo, hi in X_LOADS} for a in range(2)
+        ]
+        grouped = [keep.tile([P, TOKENS, 4], BF16, name=f"grouped{a}", align_bytes=64) for a in range(2)]
+
+        def load_x(a):
+            rows = xT[a * K_PASS : (a + 1) * K_PASS, :].rearrange("(p j) t -> p j t", j=4)
+            for lo, hi in X_LOADS:
+                nc.sync.dma_start(x_raw[a][lo][:], rows[:, :, lo:hi])
+
+        load_x(0)
+        nc.sync.dma_start(offs_t[:], offs)
+        load_x(1)
+        load_scale_rows(nc.sync, ROW0[1], w4_scales)
+        w8_dst = w8_t[:].bitcast(I32).rearrange("p (e n) -> p e n", e=EXPERTS)
+        w4_dst = w4_t[:].bitcast(I32).rearrange("p (e n) -> p e n", e=EXPERTS)
+        w8_src = w8_words.rearrange("e a p n r -> p (e a) (n r)").bitcast(I32)
+        w4_src = w4_words.rearrange("e a p n -> p (e a) n").bitcast(I32)
+        for lo in range(0, EXPERTS, 4):
+            nc.sync.dma_start(w8_dst[:, lo : lo + 4], w8_src[:, lo : lo + 4])
+            nc.sync.dma_start(w4_dst[:, lo : lo + 4], w4_src[:, lo : lo + 4])
+            if lo == 0:
+                nc.sync.dma_start(bias_t[:], b)
+            if lo == 4:
+                nc.sync.dma_start(pos1_t[:], pos1)
+            if lo == 8:
+                nc.sync.dma_start(gate_t[0][:], gate[0])
+        nc.sync.dma_start(pos2_t[:], pos2)
+        nc.sync.dma_start(gate_t[1][:], gate[1])
+
+        def interleave(a, copy, cols):
+            for lo, hi in cols:
+                start = max(first for first, last in X_LOADS if first <= lo)
+                copy(
+                    grouped[a][:, lo:hi, :].rearrange("p (c i) j -> p c j i", i=4),
+                    x_raw[a][start][:, :, lo - start : hi - start].rearrange("p j (c i) -> p c j i", i=4),
+                )
+
+        def quantize(a, u):
+            cols = slice(u * UNIT, (u + 1) * UNIT)
+            nc.vector.quantize_mx(
+                out=codes[a][:, cols].bitcast(FP8X4),
+                scales=scales[ROW0[a] :, cols],
+                in_=grouped[a][:, cols, :].rearrange("p t j -> p (t j)"),
+            )
+
+        def gather(dst, window, lo, hi):
+            nc.vector.tensor_copy(dst[:, lo:hi], window[:].indirect(offs_t[:, lo // 16 : hi // 16]))
+
+        interleave(0, nc.scalar.copy, SCALAR_COLS[0])
+        interleave(0, nc.vector.tensor_copy, VECTOR_COLS[0])
+        for u in range(TOKENS // UNIT):
+            quantize(0, u)
+        interleave(1, nc.scalar.copy, SCALAR_COLS[1])
+        gather(slot_codes[0], codes[0], 0, 768)
+        quantize(1, 0)
+        gather(slot_codes[0], codes[0], 768, 1536)
+        quantize(1, 1)
+        gather(slot_codes[0], codes[0], 1536, 2048)
+        interleave(1, nc.vector.tensor_copy, VECTOR_COLS[1])
+        for u in (2, 3, 4):
+            quantize(1, u)
+
+        banks = {lo: psum.tile([P, (hi - lo) * CAP], F32, name=f"bank{lo}") for lo, hi in GROUPS}
+        where = {e: banks[lo][:, (e - lo) * CAP : (e - lo + 1) * CAP] for lo, hi in GROUPS for e in range(lo, hi)}
+
+        def multiply(e, a):
+            cols = slice(e * CAP, (e + 1) * CAP)
+            if a == 0:
+                weights = w8_t[:, e * 4 * N : (e + 1) * 4 * N].bitcast(FP8X4)
+            else:
+                weights = w4_t[:, e * 2 * N : (e + 1) * 2 * N].bitcast(FP4X4)
+            nc.tensor.matmul_mx(
+                out=where[e],
+                lhsT=weights,
+                lhsT_scale=ws_t[ROW0[a] :, e * N : (e + 1) * N],
+                rhs=slot_codes[a][:, cols].bitcast(FP8X4),
+                rhs_scale=slot_scales[ROW0[a] :, cols],
+                start=(a == 0),
+                stop=(a == 1),
+            )
+
+        def activate(lo, hi):
+            r = keep.tile([P, (hi - lo) * CAP], F32, name=f"r{lo}")
+            for e in range(lo, hi):
+                nc.scalar.activation(
+                    r[:, (e - lo) * CAP : (e - lo + 1) * CAP],
+                    where[e],
+                    RELU,
+                    bias=bias_t[:, e : e + 1],
+                )
+            nc.scalar.activation(y[:, lo * CAP : hi * CAP], r[:], SQUARE)
+
+        def activate_vector(lo, hi):
+            r = keep.tile([P, (hi - lo) * CAP], F32, name=f"r{lo}")
+            for e in range(lo, hi):
+                nc.vector.tensor_scalar(
+                    r[:, (e - lo) * CAP : (e - lo + 1) * CAP], where[e], bias_t[:, e : e + 1], 0.0, ADD, MAX
+                )
+            nc.vector.tensor_tensor(y[:, lo * CAP : hi * CAP], r[:], r[:], MULT)
+
+        for lo, hi in ((0, 2), (2, 6), (6, 10), (10, 12), (12, 14), (14, 16)):
+            gather(slot_scales, scales, lo * CAP, hi * CAP)
+            gather(slot_codes[1], codes[1], lo * CAP, hi * CAP)
+            order = [(e, a) for e in range(lo, hi) for a in range(2)]
+            if lo >= 12:
+                order = [(e, a) for a in range(2) for e in range(lo, hi)]
+            for e, a in order:
+                multiply(e, a)
+            if lo < ON_VECTOR:
+                activate(lo, min(hi, ON_VECTOR))
+        activate_vector(ON_VECTOR, EXPERTS - 1)
+        activate_vector(EXPERTS - 1, EXPERTS)
+
+        z1 = keep.tile([P, TOKENS], F32, name="z1")
+        nc.vector.tensor_tensor(z1[:], y[:].indirect(pos1_t[:]), gate_t[0][:], MULT)
+        z2 = keep.tile([P, TOKENS], F32, name="z2")
+        o = keep.tile([P, TOKENS], F32, name="o")
+
+        def product(lo, hi):
+            nc.vector.tensor_tensor(
+                z2[:, lo:hi], y[:].indirect(pos2_t[:, lo // 16 : hi // 16]), gate_t[1][:, lo:hi], MULT
+            )
+
+        def finish(lo, hi):
+            nc.vector.tensor_tensor(o[:, lo:hi], z1[:, lo:hi], z2[:, lo:hi], ADD)
+            nc.sync.dma_start(out[:, lo:hi], o[:, lo:hi])
+
+        product(0, 704)
+        product(704, 1088)
+        finish(0, 704)
+        product(1088, 1280)
+        finish(704, 1088)
+        finish(1088, 1280)

@@ -26,19 +26,12 @@ MAX = mybir.AluOpType.max
 RELU = mybir.ActivationFunctionType.Relu
 SQUARE = mybir.ActivationFunctionType.Square
 
-UNIT = 256
-X_LOADS = ((0, 512), (512, 1024), (1024, 1280))
-VECTOR_COLS = (
-    ((256, 512), (768, 1024), (1024, 1184)),
-    ((768, 1024), (1024, 1184)),
-)
-SCALAR_COLS = (
-    ((0, 256), (512, 768), (1184, 1280)),
-    ((0, 256), (256, 512), (512, 768), (1184, 1280)),
-)
+X_LOADS = (((0, 512), (512, 1024), (1024, 1280)), ((0, 256), (256, 640), (640, 1024), (1024, 1280)))
+VECTOR_COLS = (((192, 512), (704, 1024), (1120, 1280)), ((1120, 1280),))
+SCALAR_COLS = (((0, 192), (512, 704), (1024, 1120)), ((0, 256), (256, 512), (512, 640), (640, 1024), (1024, 1120)))
+QUANT_COLS = ((0, 512), (512, 1024), (1024, 1280))
 ROW0 = (4, 0)
-GROUPS = ((0, 2), (2, 6), (6, 10), (10, 12), (12, 13), (13, 14), (14, 15), (15, 16))
-ON_VECTOR = 13
+CHUNKS = ((0, 2), (2, 6), (6, 9), (9, 12), (12, 14), (14, 16))
 
 
 def tile_moe_cap2_lin_relu2_kernel(
@@ -64,7 +57,7 @@ def tile_moe_cap2_lin_relu2_kernel(
         y = keep.tile([P, SLOTS + PAD], F32, name="y")
 
         nc.vector.memset(ws_t[:].bitcast(I32), 0)
-        nc.gpsimd.memset(scales[:], 0)
+        nc.vector.memset(scales[:].bitcast(I32), 0)
         ws_i32 = ws_t[:].bitcast(I32).rearrange("p (e n) -> p e n", e=EXPERTS)
 
         def load_scale_rows(queue, row0, src):
@@ -73,16 +66,19 @@ def tile_moe_cap2_lin_relu2_kernel(
                 queue.dma_start(ws_i32[32 * quad + row0 : 32 * quad + row0 + 4], rows[4 * quad : 4 * quad + 4])
 
         load_scale_rows(nc.gpsimd, ROW0[0], w8_scales)
-        nc.gpsimd.memset(y[:, SLOTS:], 0.0)
+        nc.vector.memset(y[:, SLOTS:], 0.0)
 
         x_raw = [
-            {lo: keep.tile([P, 4, hi - lo], F32, name=f"raw{a}_{lo}") for lo, hi in X_LOADS} for a in range(2)
+            {lo: keep.tile([P, 4, hi - lo], F32, name=f"raw{a}_{lo}") for lo, hi in X_LOADS[a]} for a in range(2)
         ]
-        grouped = [keep.tile([P, TOKENS, 4], BF16, name=f"grouped{a}", align_bytes=64) for a in range(2)]
+        grouped = [
+            {lo: keep.tile([P, hi - lo, 4], BF16, name=f"grouped{a}_{lo}", align_bytes=64) for lo, hi in QUANT_COLS}
+            for a in range(2)
+        ]
 
         def load_x(a):
             rows = xT[a * K_PASS : (a + 1) * K_PASS, :].rearrange("(p j) t -> p j t", j=4)
-            for lo, hi in X_LOADS:
+            for lo, hi in X_LOADS[a]:
                 nc.sync.dma_start(x_raw[a][lo][:], rows[:, :, lo:hi])
 
         load_x(0)
@@ -98,27 +94,26 @@ def tile_moe_cap2_lin_relu2_kernel(
             nc.sync.dma_start(w4_dst[:, lo : lo + 4], w4_src[:, lo : lo + 4])
             if lo == 0:
                 nc.sync.dma_start(bias_t[:], b)
-            if lo == 4:
-                nc.sync.dma_start(pos1_t[:], pos1)
-            if lo == 8:
-                nc.sync.dma_start(gate_t[0][:], gate[0])
+        nc.sync.dma_start(pos1_t[:], pos1)
+        nc.sync.dma_start(gate_t[0][:], gate[0])
         nc.sync.dma_start(pos2_t[:], pos2)
         nc.sync.dma_start(gate_t[1][:], gate[1])
 
         def interleave(a, copy, cols):
             for lo, hi in cols:
-                start = max(first for first, last in X_LOADS if first <= lo)
+                start = max(first for first, last in X_LOADS[a] if first <= lo)
+                unit = max(first for first, last in QUANT_COLS if first <= lo)
                 copy(
-                    grouped[a][:, lo:hi, :].rearrange("p (c i) j -> p c j i", i=4),
+                    grouped[a][unit][:, lo - unit : hi - unit, :].rearrange("p (c i) j -> p c j i", i=4),
                     x_raw[a][start][:, :, lo - start : hi - start].rearrange("p j (c i) -> p c j i", i=4),
                 )
 
         def quantize(a, u):
-            cols = slice(u * UNIT, (u + 1) * UNIT)
+            cols = slice(*QUANT_COLS[u])
             nc.vector.quantize_mx(
                 out=codes[a][:, cols].bitcast(FP8X4),
                 scales=scales[ROW0[a] :, cols],
-                in_=grouped[a][:, cols, :].rearrange("p t j -> p (t j)"),
+                in_=grouped[a][cols.start][:].rearrange("p t j -> p (t j)"),
             )
 
         def gather(dst, window, lo, hi):
@@ -126,24 +121,22 @@ def tile_moe_cap2_lin_relu2_kernel(
 
         interleave(0, nc.scalar.copy, SCALAR_COLS[0])
         interleave(0, nc.vector.tensor_copy, VECTOR_COLS[0])
-        for u in range(TOKENS // UNIT):
+        for u in range(len(QUANT_COLS)):
             quantize(0, u)
         interleave(1, nc.scalar.copy, SCALAR_COLS[1])
-        gather(slot_codes[0], codes[0], 0, 768)
+        for lo, hi in ((0, 768), (768, 1408), (1408, 2048)):
+            gather(slot_codes[0], codes[0], lo, hi)
         quantize(1, 0)
-        gather(slot_codes[0], codes[0], 768, 1536)
-        quantize(1, 1)
-        gather(slot_codes[0], codes[0], 1536, 2048)
         interleave(1, nc.vector.tensor_copy, VECTOR_COLS[1])
-        for u in (2, 3, 4):
-            quantize(1, u)
+        quantize(1, 1)
+        quantize(1, 2)
 
-        banks = {lo: psum.tile([P, (hi - lo) * CAP], F32, name=f"bank{lo}") for lo, hi in GROUPS}
-        where = {e: banks[lo][:, (e - lo) * CAP : (e - lo + 1) * CAP] for lo, hi in GROUPS for e in range(lo, hi)}
+        where = {}
 
         def multiply(e, a):
             cols = slice(e * CAP, (e + 1) * CAP)
             if a == 0:
+                where[e] = psum.tile([P, CAP], F32, name="bank", bufs=8)[:]
                 weights = w8_t[:, e * 4 * N : (e + 1) * 4 * N].bitcast(FP8X4)
             else:
                 weights = w4_t[:, e * 2 * N : (e + 1) * 2 * N].bitcast(FP4X4)
@@ -157,8 +150,9 @@ def tile_moe_cap2_lin_relu2_kernel(
                 stop=(a == 1),
             )
 
+        r = keep.tile([P, 4 * CAP], F32, name="r")
+
         def activate(lo, hi):
-            r = keep.tile([P, (hi - lo) * CAP], F32, name=f"r{lo}")
             for e in range(lo, hi):
                 nc.scalar.activation(
                     r[:, (e - lo) * CAP : (e - lo + 1) * CAP],
@@ -166,7 +160,7 @@ def tile_moe_cap2_lin_relu2_kernel(
                     RELU,
                     bias=bias_t[:, e : e + 1],
                 )
-            nc.scalar.activation(y[:, lo * CAP : hi * CAP], r[:], SQUARE)
+            nc.scalar.activation(y[:, lo * CAP : hi * CAP], r[:, : (hi - lo) * CAP], SQUARE)
 
         def activate_vector(lo, hi):
             r = keep.tile([P, (hi - lo) * CAP], F32, name=f"r{lo}")
@@ -176,17 +170,13 @@ def tile_moe_cap2_lin_relu2_kernel(
                 )
             nc.vector.tensor_tensor(y[:, lo * CAP : hi * CAP], r[:], r[:], MULT)
 
-        for lo, hi in ((0, 2), (2, 6), (6, 10), (10, 12), (12, 14), (14, 16)):
+        for lo, hi in CHUNKS:
             gather(slot_scales, scales, lo * CAP, hi * CAP)
             gather(slot_codes[1], codes[1], lo * CAP, hi * CAP)
-            order = [(e, a) for e in range(lo, hi) for a in range(2)]
-            if lo >= 12:
-                order = [(e, a) for a in range(2) for e in range(lo, hi)]
-            for e, a in order:
-                multiply(e, a)
-            if lo < ON_VECTOR:
-                activate(lo, min(hi, ON_VECTOR))
-        activate_vector(ON_VECTOR, EXPERTS - 1)
+            for a in range(2):
+                for e in range(lo, hi):
+                    multiply(e, a)
+            activate(lo, min(hi, EXPERTS - 1))
         activate_vector(EXPERTS - 1, EXPERTS)
 
         z1 = keep.tile([P, TOKENS], F32, name="z1")

@@ -1,6 +1,7 @@
 from contextlib import ExitStack
 
 import concourse.mybir as mybir
+from concourse.masks import make_identity
 
 P = 128
 TOKENS = 1280
@@ -30,8 +31,9 @@ X_LOADS = (((0, 512), (512, 1024), (1024, 1280)), ((0, 256), (256, 640), (640, 1
 VECTOR_COLS = (((192, 512), (704, 1024), (1120, 1280)), ((1120, 1280),))
 SCALAR_COLS = (((0, 192), (512, 704), (1024, 1120)), ((0, 256), (256, 512), (512, 640), (640, 1024), (1024, 1120)))
 QUANT_COLS = ((0, 512), (512, 1024), (1024, 1280))
+SPLIT = 640
 ROW0 = (4, 0)
-CHUNKS = ((0, 2), (2, 6), (6, 9), (9, 12), (12, 14), (14, 16))
+W_LOADS = ((0, 4), (4, 8), (8, 12), (12, 16))
 
 
 def tile_moe_cap2_lin_relu2_kernel(
@@ -46,9 +48,9 @@ def tile_moe_cap2_lin_relu2_kernel(
         pos1_t = keep.tile([P, TOKENS // 16], U16, name="pos1_t")
         pos2_t = keep.tile([P, TOKENS // 16], U16, name="pos2_t")
         bias_t = keep.tile([P, EXPERTS], F32, name="bias_t")
-        gate_t = [keep.tile([P, TOKENS], F32, name=f"gate{c}") for c in range(2)]
-        w8_t = keep.tile([P, EXPERTS * 4 * N], U8, name="w8_t", align_bytes=64)
-        w4_t = keep.tile([P, EXPERTS * 2 * N], U8, name="w4_t", align_bytes=64)
+        gate_t = {lo: keep.tile([P, 2, hi - lo], F32, name=f"gate{lo}") for lo, hi in ((0, SPLIT), (SPLIT, TOKENS))}
+        w8_t = {lo: keep.tile([P, (hi - lo) * 4 * N], U8, name=f"w8_{lo}", align_bytes=64) for lo, hi in W_LOADS}
+        w4_t = {lo: keep.tile([P, (hi - lo) * 2 * N], U8, name=f"w4_{lo}", align_bytes=64) for lo, hi in W_LOADS}
         ws_t = keep.tile([P, EXPERTS * N], U8, name="ws_t", align_bytes=64)
         codes = [keep.tile([P, TOKENS], U32, name=f"codes{a}", align_bytes=64) for a in range(2)]
         scales = keep.tile([P, TOKENS], U8, name="scales", align_bytes=64)
@@ -56,7 +58,7 @@ def tile_moe_cap2_lin_relu2_kernel(
         slot_scales = keep.tile([P, SLOTS], U8, name="slot_scales", align_bytes=64)
         y = keep.tile([P, SLOTS + PAD], F32, name="y")
 
-        nc.vector.memset(ws_t[:].bitcast(I32), 0)
+        nc.gpsimd.memset(ws_t[:].bitcast(I32), 0)
         nc.vector.memset(scales[:].bitcast(I32), 0)
         ws_i32 = ws_t[:].bitcast(I32).rearrange("p (e n) -> p e n", e=EXPERTS)
 
@@ -66,6 +68,8 @@ def tile_moe_cap2_lin_relu2_kernel(
                 queue.dma_start(ws_i32[32 * quad + row0 : 32 * quad + row0 + 4], rows[4 * quad : 4 * quad + 4])
 
         load_scale_rows(nc.gpsimd, ROW0[0], w8_scales)
+        ident = keep.tile([P, P], F32, name="ident")
+        make_identity(nc, ident[:])
         nc.vector.memset(y[:, SLOTS:], 0.0)
 
         x_raw = [
@@ -85,19 +89,17 @@ def tile_moe_cap2_lin_relu2_kernel(
         nc.sync.dma_start(offs_t[:], offs)
         load_x(1)
         load_scale_rows(nc.sync, ROW0[1], w4_scales)
-        w8_dst = w8_t[:].bitcast(I32).rearrange("p (e n) -> p e n", e=EXPERTS)
-        w4_dst = w4_t[:].bitcast(I32).rearrange("p (e n) -> p e n", e=EXPERTS)
         w8_src = w8_words.rearrange("e a p n r -> p (e a) (n r)").bitcast(I32)
         w4_src = w4_words.rearrange("e a p n -> p (e a) n").bitcast(I32)
-        for lo in range(0, EXPERTS, 4):
-            nc.sync.dma_start(w8_dst[:, lo : lo + 4], w8_src[:, lo : lo + 4])
-            nc.sync.dma_start(w4_dst[:, lo : lo + 4], w4_src[:, lo : lo + 4])
+        for lo, hi in W_LOADS:
+            nc.sync.dma_start(w4_t[lo][:].bitcast(I32).rearrange("p (e n) -> p e n", e=hi - lo), w4_src[:, lo:hi])
+            nc.sync.dma_start(w8_t[lo][:].bitcast(I32).rearrange("p (e n) -> p e n", e=hi - lo), w8_src[:, lo:hi])
             if lo == 0:
                 nc.sync.dma_start(bias_t[:], b)
         nc.sync.dma_start(pos1_t[:], pos1)
-        nc.sync.dma_start(gate_t[0][:], gate[0])
         nc.sync.dma_start(pos2_t[:], pos2)
-        nc.sync.dma_start(gate_t[1][:], gate[1])
+        for lo, hi in ((0, SPLIT), (SPLIT, TOKENS)):
+            nc.sync.dma_start(gate_t[lo][:], gate[:, :, lo:hi].rearrange("c n t -> n c t"))
 
         def interleave(a, copy, cols):
             for lo, hi in cols:
@@ -133,13 +135,14 @@ def tile_moe_cap2_lin_relu2_kernel(
 
         where = {}
 
-        def multiply(e, a):
+        def multiply(e, a, bank):
             cols = slice(e * CAP, (e + 1) * CAP)
+            first = max(lo for lo, hi in W_LOADS if lo <= e)
             if a == 0:
-                where[e] = psum.tile([P, CAP], F32, name="bank", bufs=8)[:]
-                weights = w8_t[:, e * 4 * N : (e + 1) * 4 * N].bitcast(FP8X4)
+                where[e] = psum.tile([P, CAP], F32, name=f"bank{bank}")[:]
+                weights = w8_t[first][:, (e - first) * 4 * N : (e - first + 1) * 4 * N].bitcast(FP8X4)
             else:
-                weights = w4_t[:, e * 2 * N : (e + 1) * 2 * N].bitcast(FP4X4)
+                weights = w4_t[first][:, (e - first) * 2 * N : (e - first + 1) * 2 * N].bitcast(FP4X4)
             nc.tensor.matmul_mx(
                 out=where[e],
                 lhsT=weights,
@@ -155,12 +158,12 @@ def tile_moe_cap2_lin_relu2_kernel(
         def activate(lo, hi):
             for e in range(lo, hi):
                 nc.scalar.activation(
-                    r[:, (e - lo) * CAP : (e - lo + 1) * CAP],
+                    r[:, e % 4 * CAP : (e % 4 + 1) * CAP],
                     where[e],
                     RELU,
                     bias=bias_t[:, e : e + 1],
                 )
-            nc.scalar.activation(y[:, lo * CAP : hi * CAP], r[:, : (hi - lo) * CAP], SQUARE)
+            nc.scalar.activation(y[:, lo * CAP : hi * CAP], r[:, lo % 4 * CAP : ((hi - 1) % 4 + 1) * CAP], SQUARE)
 
         def activate_vector(lo, hi):
             r = keep.tile([P, (hi - lo) * CAP], F32, name=f"r{lo}")
@@ -170,32 +173,62 @@ def tile_moe_cap2_lin_relu2_kernel(
                 )
             nc.vector.tensor_tensor(y[:, lo * CAP : hi * CAP], r[:], r[:], MULT)
 
-        for lo, hi in CHUNKS:
+        for lo, hi in W_LOADS:
             gather(slot_scales, scales, lo * CAP, hi * CAP)
-            gather(slot_codes[1], codes[1], lo * CAP, hi * CAP)
-            for a in range(2):
-                for e in range(lo, hi):
-                    multiply(e, a)
-            activate(lo, min(hi, EXPERTS - 1))
+            for e in range(lo, hi):
+                multiply(e, 0, e % 4)
+            for first, last in ((lo, hi),) if hi < EXPERTS else ((lo, lo + 2), (lo + 2, hi)):
+                gather(slot_codes[1], codes[1], first * CAP, last * CAP)
+                for e in range(first, last):
+                    multiply(e, 1, None)
+                activate(first, min(last, EXPERTS - 1))
         activate_vector(EXPERTS - 1, EXPERTS)
 
-        z1 = keep.tile([P, TOKENS], F32, name="z1")
-        nc.vector.tensor_tensor(z1[:], y[:].indirect(pos1_t[:]), gate_t[0][:], MULT)
-        z2 = keep.tile([P, TOKENS], F32, name="z2")
+        z = [keep.tile([P, TOKENS], F32, name=f"z{c}") for c in range(2)]
         o = keep.tile([P, TOKENS], F32, name="o")
+        pos_t = (pos1_t, pos2_t)
 
-        def product(lo, hi):
+        def product(c, lo, hi):
+            first = 0 if lo < SPLIT else SPLIT
             nc.vector.tensor_tensor(
-                z2[:, lo:hi], y[:].indirect(pos2_t[:, lo // 16 : hi // 16]), gate_t[1][:, lo:hi], MULT
+                z[c][:, lo:hi],
+                y[:].indirect(pos_t[c][:, lo // 16 : hi // 16]),
+                gate_t[first][:, c, lo - first : hi - first],
+                MULT,
             )
 
-        def finish(lo, hi):
-            nc.vector.tensor_tensor(o[:, lo:hi], z1[:, lo:hi], z2[:, lo:hi], ADD)
+        def add_on_tensor(lo, hi):
+            turned = psum.tile([P, hi - lo], F32, name=f"turned{lo}")
+            for t in range(lo, hi, P):
+                for c in range(2):
+                    nc.tensor.matmul(
+                        turned[:, t - lo : t - lo + P],
+                        z[c][:, t : t + P],
+                        ident[:],
+                        start=(c == 0),
+                        stop=(c == 1),
+                        is_transpose=True,
+                    )
+            total = keep.tile([P, hi - lo], F32, name=f"total{lo}")
+            nc.scalar.copy(total[:], turned[:])
+            back = psum.tile([P, hi - lo], F32, name=f"back{lo}")
+            for t in range(0, hi - lo, P):
+                nc.tensor.transpose(back[:, t : t + P], total[:, t : t + P], ident[:])
+            nc.scalar.copy(o[:, lo:hi], back[:])
+            nc.scalar.dma_start(out[:, lo:hi], o[:, lo:hi])
+
+        def add_on_vector(lo, hi):
+            nc.vector.tensor_tensor(o[:, lo:hi], z[0][:, lo:hi], z[1][:, lo:hi], ADD)
             nc.sync.dma_start(out[:, lo:hi], o[:, lo:hi])
 
-        product(0, 704)
-        product(704, 1088)
-        finish(0, 704)
-        product(1088, 1280)
-        finish(704, 1088)
-        finish(1088, 1280)
+        for lo, hi in ((0, 384), (384, SPLIT)):
+            product(0, lo, hi)
+            product(1, lo, hi)
+            add_on_tensor(lo, hi)
+        product(0, SPLIT, TOKENS)
+        product(1, SPLIT, 960)
+        product(1, 960, 1152)
+        add_on_vector(SPLIT, 960)
+        product(1, 1152, 1280)
+        add_on_vector(960, 1152)
+        add_on_vector(1152, 1280)

@@ -67,7 +67,6 @@ def tile_moe_cap2_lin_relu2_kernel(
             for quad in range(4):
                 queue.dma_start(ws_i32[32 * quad + row0 : 32 * quad + row0 + 4], rows[4 * quad : 4 * quad + 4])
 
-        load_scale_rows(nc.gpsimd, ROW0[0], w8_scales)
         ident = keep.tile([P, P], F32, name="ident")
         make_identity(nc, ident[:])
         nc.vector.memset(y[:, SLOTS:], 0.0)
@@ -88,6 +87,7 @@ def tile_moe_cap2_lin_relu2_kernel(
         load_x(0)
         nc.sync.dma_start(offs_t[:], offs)
         load_x(1)
+        load_scale_rows(nc.sync, ROW0[0], w8_scales)
         load_scale_rows(nc.sync, ROW0[1], w4_scales)
         w8_src = w8_words.rearrange("e a p n r -> p (e a) (n r)").bitcast(I32)
         w4_src = w4_words.rearrange("e a p n -> p (e a) n").bitcast(I32)

@@ -27,10 +27,13 @@ MAX = mybir.AluOpType.max
 RELU = mybir.ActivationFunctionType.Relu
 SQUARE = mybir.ActivationFunctionType.Square
 
-X_LOADS = (((0, 512), (512, 1024), (1024, 1280)), ((0, 256), (256, 640), (640, 1024), (1024, 1280)))
-VECTOR_COLS = (((192, 512), (704, 1024), (1120, 1280)), ((1120, 1280),))
-SCALAR_COLS = (((0, 192), (512, 704), (1024, 1120)), ((0, 256), (256, 512), (512, 640), (640, 1024), (1024, 1120)))
-QUANT_COLS = ((0, 512), (512, 1024), (1024, 1280))
+X_LOADS = (((0, 768), (768, 1280)), ((0, 512), (512, 1024), (1024, 1280)))
+VECTOR_COLS = (((0, 512), (768, 1024), (1184, 1280)), ((1088, 1280),))
+SCALAR_COLS = (((512, 768), (1024, 1184)), ((0, 512), (512, 768), (768, 1024), (1024, 1088)))
+QUANT_COLS = (
+    ((0, 512), (512, 768), (768, 1024), (1024, 1280)),
+    ((0, 512), (512, 768), (768, 1024), (1024, 1280)),
+)
 SPLIT = 640
 ROW0 = (4, 0)
 W_LOADS = ((0, 4), (4, 8), (8, 12), (12, 16))
@@ -75,7 +78,7 @@ def tile_moe_cap2_lin_relu2_kernel(
             {lo: keep.tile([P, 4, hi - lo], F32, name=f"raw{a}_{lo}") for lo, hi in X_LOADS[a]} for a in range(2)
         ]
         grouped = [
-            {lo: keep.tile([P, hi - lo, 4], BF16, name=f"grouped{a}_{lo}", align_bytes=64) for lo, hi in QUANT_COLS}
+            {lo: keep.tile([P, hi - lo, 4], BF16, name=f"grouped{a}_{lo}", align_bytes=64) for lo, hi in QUANT_COLS[a]}
             for a in range(2)
         ]
 
@@ -104,14 +107,14 @@ def tile_moe_cap2_lin_relu2_kernel(
         def interleave(a, copy, cols):
             for lo, hi in cols:
                 start = max(first for first, last in X_LOADS[a] if first <= lo)
-                unit = max(first for first, last in QUANT_COLS if first <= lo)
+                unit = max(first for first, last in QUANT_COLS[a] if first <= lo)
                 copy(
                     grouped[a][unit][:, lo - unit : hi - unit, :].rearrange("p (c i) j -> p c j i", i=4),
                     x_raw[a][start][:, :, lo - start : hi - start].rearrange("p j (c i) -> p c j i", i=4),
                 )
 
         def quantize(a, u):
-            cols = slice(*QUANT_COLS[u])
+            cols = slice(*QUANT_COLS[a][u])
             nc.vector.quantize_mx(
                 out=codes[a][:, cols].bitcast(FP8X4),
                 scales=scales[ROW0[a] :, cols],
@@ -123,7 +126,7 @@ def tile_moe_cap2_lin_relu2_kernel(
 
         interleave(0, nc.scalar.copy, SCALAR_COLS[0])
         interleave(0, nc.vector.tensor_copy, VECTOR_COLS[0])
-        for u in range(len(QUANT_COLS)):
+        for u in range(len(QUANT_COLS[0])):
             quantize(0, u)
         interleave(1, nc.scalar.copy, SCALAR_COLS[1])
         for lo, hi in ((0, 768), (768, 1408), (1408, 2048)):
@@ -132,6 +135,7 @@ def tile_moe_cap2_lin_relu2_kernel(
         interleave(1, nc.vector.tensor_copy, VECTOR_COLS[1])
         quantize(1, 1)
         quantize(1, 2)
+        quantize(1, 3)
 
         where = {}
 

@@ -177,15 +177,14 @@ def tile_moe_cap2_lin_relu2_kernel(
                 )
             nc.vector.tensor_tensor(y[:, lo * CAP : hi * CAP], r[:], r[:], MULT)
 
-        for lo, hi in W_LOADS:
+        for lo, hi in ((0, 4), (4, 8), (8, 12), (12, 14), (14, 16)):
             gather(slot_scales, scales, lo * CAP, hi * CAP)
             for e in range(lo, hi):
                 multiply(e, 0, e % 4)
-            for first, last in ((lo, hi),) if hi < EXPERTS else ((lo, lo + 2), (lo + 2, hi)):
-                gather(slot_codes[1], codes[1], first * CAP, last * CAP)
-                for e in range(first, last):
-                    multiply(e, 1, None)
-                activate(first, min(last, EXPERTS - 1))
+            gather(slot_codes[1], codes[1], lo * CAP, hi * CAP)
+            for e in range(lo, hi):
+                multiply(e, 1, None)
+            activate(lo, min(hi, EXPERTS - 1))
         activate_vector(EXPERTS - 1, EXPERTS)
 
         z = [keep.tile([P, TOKENS], F32, name=f"z{c}") for c in range(2)]
@@ -229,10 +228,11 @@ def tile_moe_cap2_lin_relu2_kernel(
             product(0, lo, hi)
             product(1, lo, hi)
             add_on_tensor(lo, hi)
-        product(0, SPLIT, TOKENS)
+        product(0, SPLIT, 960)
         product(1, SPLIT, 960)
-        product(1, 960, 1152)
+        product(0, 960, TOKENS)
         add_on_vector(SPLIT, 960)
+        product(1, 960, 1152)
         product(1, 1152, 1280)
         add_on_vector(960, 1152)
         add_on_vector(1152, 1280)

@@ -27,16 +27,24 @@ MAX = mybir.AluOpType.max
 RELU = mybir.ActivationFunctionType.Relu
 SQUARE = mybir.ActivationFunctionType.Square
 
-X_LOADS = (((0, 768), (768, 1280)), ((0, 512), (512, 1024), (1024, 1280)))
-VECTOR_COLS = (((0, 512), (768, 1024), (1184, 1280)), ((1088, 1280),))
-SCALAR_COLS = (((512, 768), (1024, 1184)), ((0, 512), (512, 768), (768, 1024), (1024, 1088)))
-QUANT_COLS = (
-    ((0, 512), (512, 768), (768, 1024), (1024, 1280)),
-    ((0, 512), (512, 768), (768, 1024), (1024, 1280)),
-)
+LATE_LOADS0 = ((0, 768), (768, 1280))
+EARLY_ON_VECTOR0 = 832
+LATE_ON_VECTOR0 = ((0, 256), (256, 320), (768, 1056))
+LATE_ON_SCALAR0 = ((320, 512), (512, 768), (1056, 1280))
+UNITS0 = ((0, 256), (256, 512), (512, 768), (768, 1024), (1024, 1280))
+LOADS1 = ((0, 512), (512, 1024), (1024, 1280))
+ON_SCALAR1 = ((0, 320), (512, 800), (1024, 1152))
+ON_GPSIMD1 = ((320, 512), (800, 1024))
+ON_VECTOR1 = (1152, 1280)
+EARLY_SLOTS = 1152
 SPLIT = 640
 ROW0 = (4, 0)
 W_LOADS = ((0, 4), (4, 8), (8, 12), (12, 16))
+GROUPS = ((0, 4), (4, 8), (8, 12), (12, 14), (14, 16))
+
+
+def start_of(ranges, col):
+    return max(lo for lo, hi in ranges if lo <= col)
 
 
 def tile_moe_cap2_lin_relu2_kernel(
@@ -48,50 +56,43 @@ def tile_moe_cap2_lin_relu2_kernel(
         psum = ctx.enter_context(tc.psum_pool(name="psum", bufs=1))
 
         offs_t = keep.tile([P, SLOTS // 16], U16, name="offs_t")
-        pos1_t = keep.tile([P, TOKENS // 16], U16, name="pos1_t")
-        pos2_t = keep.tile([P, TOKENS // 16], U16, name="pos2_t")
+        pos_t = [keep.tile([P, TOKENS // 16], U16, name=f"pos{c}_t") for c in range(2)]
         bias_t = keep.tile([P, EXPERTS], F32, name="bias_t")
-        gate_t = {lo: keep.tile([P, 2, hi - lo], F32, name=f"gate{lo}") for lo, hi in ((0, SPLIT), (SPLIT, TOKENS))}
+        gate_t = keep.tile([P, 2, TOKENS], F32, name="gate_t")
         w8_t = {lo: keep.tile([P, (hi - lo) * 4 * N], U8, name=f"w8_{lo}", align_bytes=64) for lo, hi in W_LOADS}
         w4_t = {lo: keep.tile([P, (hi - lo) * 2 * N], U8, name=f"w4_{lo}", align_bytes=64) for lo, hi in W_LOADS}
         ws_t = keep.tile([P, EXPERTS * N], U8, name="ws_t", align_bytes=64)
         codes = [keep.tile([P, TOKENS], U32, name=f"codes{a}", align_bytes=64) for a in range(2)]
         scales = keep.tile([P, TOKENS], U8, name="scales", align_bytes=64)
-        slot_codes = [keep.tile([P, SLOTS], U32, name=f"slot_codes{a}", align_bytes=64) for a in range(2)]
+        early_words = keep.tile([P, EARLY_SLOTS], U32, name="early_words", align_bytes=64)
+        words1 = keep.tile([P, SLOTS], U32, name="words1", align_bytes=64)
         slot_scales = keep.tile([P, SLOTS], U8, name="slot_scales", align_bytes=64)
         y = keep.tile([P, SLOTS + PAD], F32, name="y")
+        ident = keep.tile([P, P], F32, name="ident")
+        grouped = [keep.tile([P, TOKENS, 4], BF16, name=f"grouped{a}", align_bytes=64) for a in range(2)]
+        early0 = keep.tile([P, 2, TOKENS], F32, name="early0")
+        late0 = {lo: keep.tile([P, 2, hi - lo], F32, name=f"late0_{lo}") for lo, hi in LATE_LOADS0}
+        raw1 = {lo: keep.tile([P, 4, hi - lo], F32, name=f"raw1_{lo}", align_bytes=64) for lo, hi in LOADS1}
 
         nc.gpsimd.memset(ws_t[:].bitcast(I32), 0)
         nc.vector.memset(scales[:].bitcast(I32), 0)
-        ws_i32 = ws_t[:].bitcast(I32).rearrange("p (e n) -> p e n", e=EXPERTS)
-
-        def load_scale_rows(queue, row0, src):
-            rows = src.rearrange("e a q n -> q (e a) n").bitcast(I32)
-            for quad in range(4):
-                queue.dma_start(ws_i32[32 * quad + row0 : 32 * quad + row0 + 4], rows[4 * quad : 4 * quad + 4])
-
-        ident = keep.tile([P, P], F32, name="ident")
         make_identity(nc, ident[:])
         nc.vector.memset(y[:, SLOTS:], 0.0)
 
-        x_raw = [
-            {lo: keep.tile([P, 4, hi - lo], F32, name=f"raw{a}_{lo}") for lo, hi in X_LOADS[a]} for a in range(2)
-        ]
-        grouped = [
-            {lo: keep.tile([P, hi - lo, 4], BF16, name=f"grouped{a}_{lo}", align_bytes=64) for lo, hi in QUANT_COLS[a]}
-            for a in range(2)
-        ]
-
-        def load_x(a):
-            rows = xT[a * K_PASS : (a + 1) * K_PASS, :].rearrange("(p j) t -> p j t", j=4)
-            for lo, hi in X_LOADS[a]:
-                nc.sync.dma_start(x_raw[a][lo][:], rows[:, :, lo:hi])
-
-        load_x(0)
+        rows = [xT[a * K_PASS : (a + 1) * K_PASS, :].rearrange("(p j) t -> p j t", j=4) for a in range(2)]
+        nc.sync.dma_start(early0[:], rows[0][:, 0:2, :])
+        for lo, hi in LATE_LOADS0:
+            nc.sync.dma_start(late0[lo][:], rows[0][:, 2:4, lo:hi])
         nc.sync.dma_start(offs_t[:], offs)
-        load_x(1)
-        load_scale_rows(nc.sync, ROW0[0], w8_scales)
-        load_scale_rows(nc.sync, ROW0[1], w4_scales)
+        for lo, hi in LOADS1:
+            nc.sync.dma_start(raw1[lo][:], rows[1][:, :, lo:hi])
+        ws_i32 = ws_t[:].bitcast(I32).rearrange("p (e n) -> p e n", e=EXPERTS)
+        for row0, src in zip(ROW0, (w8_scales, w4_scales)):
+            scale_rows = src.rearrange("e a q n -> q (e a) n").bitcast(I32)
+            for quad in range(4):
+                nc.sync.dma_start(
+                    ws_i32[32 * quad + row0 : 32 * quad + row0 + 4], scale_rows[4 * quad : 4 * quad + 4]
+                )
         w8_src = w8_words.rearrange("e a p n r -> p (e a) (n r)").bitcast(I32)
         w4_src = w4_words.rearrange("e a p n -> p (e a) n").bitcast(I32)
         for lo, hi in W_LOADS:
@@ -99,104 +100,114 @@ def tile_moe_cap2_lin_relu2_kernel(
             nc.sync.dma_start(w8_t[lo][:].bitcast(I32).rearrange("p (e n) -> p e n", e=hi - lo), w8_src[:, lo:hi])
             if lo == 0:
                 nc.sync.dma_start(bias_t[:], b)
-        nc.sync.dma_start(pos1_t[:], pos1)
-        nc.sync.dma_start(pos2_t[:], pos2)
-        for lo, hi in ((0, SPLIT), (SPLIT, TOKENS)):
-            nc.sync.dma_start(gate_t[lo][:], gate[:, :, lo:hi].rearrange("c n t -> n c t"))
+        nc.sync.dma_start(pos_t[0][:], pos1)
+        nc.sync.dma_start(pos_t[1][:], pos2)
+        nc.sync.dma_start(gate_t[:], gate.rearrange("c n t -> n c t"))
 
-        def interleave(a, copy, cols):
-            for lo, hi in cols:
-                start = max(first for first, last in X_LOADS[a] if first <= lo)
-                unit = max(first for first, last in QUANT_COLS[a] if first <= lo)
-                copy(
-                    grouped[a][unit][:, lo - unit : hi - unit, :].rearrange("p (c i) j -> p c j i", i=4),
-                    x_raw[a][start][:, :, lo - start : hi - start].rearrange("p j (c i) -> p c j i", i=4),
-                )
+        def round_early(copy, lo, hi):
+            copy(grouped[0][:, lo:hi, 0:2], early0[:, :, lo:hi].rearrange("p j t -> p t j"))
 
-        def quantize(a, u):
-            cols = slice(*QUANT_COLS[a][u])
+        def round_late(copy, lo, hi):
+            first = start_of(LATE_LOADS0, lo)
+            copy(grouped[0][:, lo:hi, 2:4], late0[first][:, :, lo - first : hi - first].rearrange("p j t -> p t j"))
+
+        def round_by_fours(copy, lo, hi):
+            first = start_of(LOADS1, lo)
+            copy(
+                grouped[1][:, lo:hi, :].rearrange("p (c i) j -> p c j i", i=4),
+                raw1[first][:, :, lo - first : hi - first].rearrange("p j (c i) -> p c j i", i=4),
+            )
+
+        def round_by_token(lo, hi):
+            first = start_of(LOADS1, lo)
+            nc.gpsimd.tensor_copy(
+                grouped[1][:, lo:hi, :], raw1[first][:, :, lo - first : hi - first].rearrange("p j t -> p t j")
+            )
+
+        def quantize(a, lo, hi):
             nc.vector.quantize_mx(
-                out=codes[a][:, cols].bitcast(FP8X4),
-                scales=scales[ROW0[a] :, cols],
-                in_=grouped[a][cols.start][:].rearrange("p t j -> p (t j)"),
+                out=codes[a][:, lo:hi].bitcast(FP8X4),
+                scales=scales[ROW0[a] :, lo:hi],
+                in_=grouped[a][:, lo:hi, :].rearrange("p t j -> p (t j)"),
             )
 
         def gather(dst, window, lo, hi):
-            nc.vector.tensor_copy(dst[:, lo:hi], window[:].indirect(offs_t[:, lo // 16 : hi // 16]))
+            nc.vector.tensor_copy(dst, window[:].indirect(offs_t[:, lo // 16 : hi // 16]))
 
-        interleave(0, nc.scalar.copy, SCALAR_COLS[0])
-        interleave(0, nc.vector.tensor_copy, VECTOR_COLS[0])
-        for u in range(len(QUANT_COLS[0])):
-            quantize(0, u)
-        interleave(1, nc.scalar.copy, SCALAR_COLS[1])
-        for lo, hi in ((0, 768), (768, 1408), (1408, 2048)):
-            gather(slot_codes[0], codes[0], lo, hi)
-        quantize(1, 0)
-        interleave(1, nc.vector.tensor_copy, VECTOR_COLS[1])
-        quantize(1, 1)
-        quantize(1, 2)
-        quantize(1, 3)
+        round_early(nc.vector.tensor_copy, 0, EARLY_ON_VECTOR0)
+        round_early(nc.scalar.copy, EARLY_ON_VECTOR0, TOKENS)
+        for lo, hi in LATE_ON_SCALAR0:
+            round_late(nc.scalar.copy, lo, hi)
+        for lo, hi in LATE_ON_VECTOR0:
+            round_late(nc.vector.tensor_copy, lo, hi)
+        for lo, hi in UNITS0:
+            quantize(0, lo, hi)
 
-        where = {}
+        for lo, hi in ON_SCALAR1:
+            round_by_fours(nc.scalar.copy, lo, hi)
+        for lo, hi in ON_GPSIMD1:
+            round_by_token(lo, hi)
+        for lo in (0, EARLY_SLOTS // 2):
+            gather(early_words[:, lo : lo + EARLY_SLOTS // 2], codes[0], lo, lo + EARLY_SLOTS // 2)
+        quantize(1, *LOADS1[0])
+        late_words = keep.tile([P, SLOTS - EARLY_SLOTS], U32, name="raw1_0", align_bytes=64)
+        gather(late_words[:], codes[0], EARLY_SLOTS, SLOTS)
+        round_by_fours(nc.vector.tensor_copy, *ON_VECTOR1)
+        quantize(1, *LOADS1[1])
+        quantize(1, *LOADS1[2])
 
-        def multiply(e, a, bank):
-            cols = slice(e * CAP, (e + 1) * CAP)
-            first = max(lo for lo, hi in W_LOADS if lo <= e)
+        sums = {}
+
+        def multiply(e, a):
+            lo, hi = e * CAP, (e + 1) * CAP
+            first = start_of(W_LOADS, e)
             if a == 0:
-                where[e] = psum.tile([P, CAP], F32, name=f"bank{bank}")[:]
+                sums[e] = psum.tile([P, CAP], F32, name=f"bank{e % 4}")[:]
                 weights = w8_t[first][:, (e - first) * 4 * N : (e - first + 1) * 4 * N].bitcast(FP8X4)
+                words = early_words[:, lo:hi] if hi <= EARLY_SLOTS else late_words[:, lo - EARLY_SLOTS : hi - EARLY_SLOTS]
             else:
                 weights = w4_t[first][:, (e - first) * 2 * N : (e - first + 1) * 2 * N].bitcast(FP4X4)
+                words = words1[:, lo:hi]
             nc.tensor.matmul_mx(
-                out=where[e],
+                out=sums[e],
                 lhsT=weights,
                 lhsT_scale=ws_t[ROW0[a] :, e * N : (e + 1) * N],
-                rhs=slot_codes[a][:, cols].bitcast(FP8X4),
-                rhs_scale=slot_scales[ROW0[a] :, cols],
+                rhs=words.bitcast(FP8X4),
+                rhs_scale=slot_scales[ROW0[a] :, lo:hi],
                 start=(a == 0),
                 stop=(a == 1),
             )
 
-        r = keep.tile([P, 4 * CAP], F32, name="r")
+        relu = keep.tile([P, 4 * CAP], F32, name="relu")
 
-        def activate(lo, hi):
+        def activate_on_scalar(lo, hi):
             for e in range(lo, hi):
-                nc.scalar.activation(
-                    r[:, e % 4 * CAP : (e % 4 + 1) * CAP],
-                    where[e],
-                    RELU,
-                    bias=bias_t[:, e : e + 1],
-                )
-            nc.scalar.activation(y[:, lo * CAP : hi * CAP], r[:, lo % 4 * CAP : ((hi - 1) % 4 + 1) * CAP], SQUARE)
+                nc.scalar.activation(relu[:, e % 4 * CAP : (e % 4 + 1) * CAP], sums[e], RELU, bias=bias_t[:, e : e + 1])
+            nc.scalar.activation(y[:, lo * CAP : hi * CAP], relu[:, lo % 4 * CAP : ((hi - 1) % 4 + 1) * CAP], SQUARE)
 
-        def activate_vector(lo, hi):
-            r = keep.tile([P, (hi - lo) * CAP], F32, name=f"r{lo}")
-            for e in range(lo, hi):
-                nc.vector.tensor_scalar(
-                    r[:, (e - lo) * CAP : (e - lo + 1) * CAP], where[e], bias_t[:, e : e + 1], 0.0, ADD, MAX
-                )
-            nc.vector.tensor_tensor(y[:, lo * CAP : hi * CAP], r[:], r[:], MULT)
+        def activate_on_vector(e):
+            relu_last = keep.tile([P, CAP], F32, name="relu_last")
+            nc.vector.tensor_scalar(relu_last[:], sums[e], bias_t[:, e : e + 1], 0.0, ADD, MAX)
+            nc.vector.tensor_tensor(y[:, e * CAP : (e + 1) * CAP], relu_last[:], relu_last[:], MULT)
 
-        for lo, hi in ((0, 4), (4, 8), (8, 12), (12, 14), (14, 16)):
-            gather(slot_scales, scales, lo * CAP, hi * CAP)
+        for lo, hi in GROUPS:
+            gather(slot_scales[:, lo * CAP : hi * CAP], scales, lo * CAP, hi * CAP)
             for e in range(lo, hi):
-                multiply(e, 0, e % 4)
-            gather(slot_codes[1], codes[1], lo * CAP, hi * CAP)
+                multiply(e, 0)
+            gather(words1[:, lo * CAP : hi * CAP], codes[1], lo * CAP, hi * CAP)
             for e in range(lo, hi):
-                multiply(e, 1, None)
-            activate(lo, min(hi, EXPERTS - 1))
-        activate_vector(EXPERTS - 1, EXPERTS)
+                multiply(e, 1)
+            activate_on_scalar(lo, min(hi, EXPERTS - 1))
+        activate_on_vector(EXPERTS - 1)
 
         z = [keep.tile([P, TOKENS], F32, name=f"z{c}") for c in range(2)]
         o = keep.tile([P, TOKENS], F32, name="o")
-        pos_t = (pos1_t, pos2_t)
 
         def product(c, lo, hi):
-            first = 0 if lo < SPLIT else SPLIT
             nc.vector.tensor_tensor(
                 z[c][:, lo:hi],
                 y[:].indirect(pos_t[c][:, lo // 16 : hi // 16]),
-                gate_t[first][:, c, lo - first : hi - first],
+                gate_t[:, c, lo:hi],
                 MULT,
             )
 
@@ -233,6 +244,6 @@ def tile_moe_cap2_lin_relu2_kernel(
         product(0, 960, TOKENS)
         add_on_vector(SPLIT, 960)
         product(1, 960, 1152)
-        product(1, 1152, 1280)
+        product(1, 1152, TOKENS)
         add_on_vector(960, 1152)
-        add_on_vector(1152, 1280)
+        add_on_vector(1152, TOKENS)

@@ -29,14 +29,14 @@ SQUARE = mybir.ActivationFunctionType.Square
 
 LATE_LOADS0 = ((0, 768), (768, 1280))
 EARLY_ON_VECTOR0 = 832
-LATE_ON_VECTOR0 = ((0, 256), (256, 320), (768, 1056))
-LATE_ON_SCALAR0 = ((320, 512), (512, 768), (1056, 1280))
+LATE_ON_VECTOR0 = ((0, 256), (256, 384), (768, 1024))
+LATE_ON_SCALAR0 = ((384, 512), (512, 768), (1024, 1280))
 UNITS0 = ((0, 256), (256, 512), (512, 768), (768, 1024), (1024, 1280))
 LOADS1 = ((0, 512), (512, 1024), (1024, 1280))
-ON_SCALAR1 = ((0, 320), (512, 800), (1024, 1152))
-ON_GPSIMD1 = ((320, 512), (800, 1024))
-ON_VECTOR1 = (1152, 1280)
-EARLY_SLOTS = 1152
+ON_SCALAR1 = ((0, 288), (512, 800), (1024, 1184))
+ON_GPSIMD1 = ((288, 512), (800, 1024))
+ON_VECTOR1 = (1184, 1280)
+EARLY_SLOTS = 1280
 SPLIT = 640
 ROW0 = (4, 0)
 W_LOADS = ((0, 4), (4, 8), (8, 12), (12, 16))

@@ -185,19 +185,32 @@ def tile_moe_cap2_lin_relu2_kernel(
                 nc.scalar.activation(relu[:, e % 4 * CAP : (e % 4 + 1) * CAP], sums[e], RELU, bias=bias_t[:, e : e + 1])
             nc.scalar.activation(y[:, lo * CAP : hi * CAP], relu[:, lo % 4 * CAP : ((hi - 1) % 4 + 1) * CAP], SQUARE)
 
+        def activate_in_halves(e):
+            halves = (slice(0, CAP // 2), slice(CAP // 2, CAP))
+            mine = relu[:, e % 4 * CAP : (e % 4 + 1) * CAP]
+            for half in halves:
+                nc.scalar.activation(mine[:, half], sums[e][:, half], RELU, bias=bias_t[:, e : e + 1])
+            for half in halves:
+                nc.scalar.activation(y[:, e * CAP : (e + 1) * CAP][:, half], mine[:, half], SQUARE)
+
         def activate_on_vector(e):
             relu_last = keep.tile([P, CAP], F32, name="relu_last")
-            nc.vector.tensor_scalar(relu_last[:], sums[e], bias_t[:, e : e + 1], 0.0, ADD, MAX)
-            nc.vector.tensor_tensor(y[:, e * CAP : (e + 1) * CAP], relu_last[:], relu_last[:], MULT)
+            halves = (slice(0, CAP // 2), slice(CAP // 2, CAP))
+            for half in halves:
+                nc.vector.tensor_scalar(relu_last[:, half], sums[e][:, half], bias_t[:, e : e + 1], 0.0, ADD, MAX)
+            for half in halves:
+                nc.vector.tensor_tensor(y[:, e * CAP : (e + 1) * CAP][:, half], relu_last[:, half], relu_last[:, half], MULT)
 
         for lo, hi in GROUPS:
             gather(slot_scales[:, lo * CAP : hi * CAP], scales, lo * CAP, hi * CAP)
             for e in range(lo, hi):
                 multiply(e, 0)
             gather(words1[:, lo * CAP : hi * CAP], codes[1], lo * CAP, hi * CAP)
-            for e in range(lo, hi):
+            for e in range(lo, hi) if hi < EXPERTS else reversed(range(lo, hi)):
                 multiply(e, 1)
-            activate_on_scalar(lo, min(hi, EXPERTS - 1))
+            if hi < EXPERTS:
+                activate_on_scalar(lo, hi)
+        activate_in_halves(EXPERTS - 2)
         activate_on_vector(EXPERTS - 1)
 
         z = [keep.tile([P, TOKENS], F32, name=f"z{c}") for c in range(2)]

@@ -1,7 +1,6 @@
 from contextlib import ExitStack
 
 import concourse.mybir as mybir
-from concourse.masks import make_identity
 
 P = 128
 TOKENS = 1280
@@ -26,6 +25,7 @@ ADD = mybir.AluOpType.add
 MAX = mybir.AluOpType.max
 RELU = mybir.ActivationFunctionType.Relu
 SQUARE = mybir.ActivationFunctionType.Square
+COPY = mybir.ActivationFunctionType.Copy
 
 LATE_LOADS0 = ((0, 768), (768, 1280))
 EARLY_ON_VECTOR0 = 832
@@ -37,8 +37,10 @@ ON_SCALAR1 = ((0, 288), (512, 800), (1024, 1184))
 ON_GPSIMD1 = ((288, 512), (800, 1024))
 ON_VECTOR1 = (1184, 1280)
 EARLY_SLOTS = 1280
-SPLIT = 640
 ROW0 = (4, 0)
+SHARED = 576
+SECOND_ONLY = ((0, 288), (288, SHARED))
+BOTH = ((SHARED, 832), (832, 1024), (1024, 1152), (1152, 1280))
 W_LOADS = ((0, 4), (4, 8), (8, 12), (12, 16))
 GROUPS = ((0, 4), (4, 8), (8, 12), (12, 14), (14, 16))
 
@@ -68,7 +70,6 @@ def tile_moe_cap2_lin_relu2_kernel(
         words1 = keep.tile([P, SLOTS], U32, name="words1", align_bytes=64)
         slot_scales = keep.tile([P, SLOTS], U8, name="slot_scales", align_bytes=64)
         y = keep.tile([P, SLOTS + PAD], F32, name="y")
-        ident = keep.tile([P, P], F32, name="ident")
         grouped = [keep.tile([P, TOKENS, 4], BF16, name=f"grouped{a}", align_bytes=64) for a in range(2)]
         early0 = keep.tile([P, 2, TOKENS], F32, name="early0")
         late0 = {lo: keep.tile([P, 2, hi - lo], F32, name=f"late0_{lo}") for lo, hi in LATE_LOADS0}
@@ -76,7 +77,6 @@ def tile_moe_cap2_lin_relu2_kernel(
 
         nc.gpsimd.memset(ws_t[:].bitcast(I32), 0)
         nc.vector.memset(scales[:].bitcast(I32), 0)
-        make_identity(nc, ident[:])
         nc.vector.memset(y[:, SLOTS:], 0.0)
 
         rows = [xT[a * K_PASS : (a + 1) * K_PASS, :].rearrange("(p j) t -> p j t", j=4) for a in range(2)]
@@ -213,50 +213,33 @@ def tile_moe_cap2_lin_relu2_kernel(
         activate_in_halves(EXPERTS - 2)
         activate_on_vector(EXPERTS - 1)
 
-        z = [keep.tile([P, TOKENS], F32, name=f"z{c}") for c in range(2)]
         o = keep.tile([P, TOKENS], F32, name="o")
+        first = keep.tile([P, SHARED], F32, name="first")
+        second = keep.tile([P, SHARED], F32, name="second")
+        fetched = {lo: keep.tile([P, hi - lo], F32, name=f"fetched{lo}") for lo, hi in SECOND_ONLY}
+        for lo, hi in BOTH:
+            fetched[lo] = keep.tile([P, 2, hi - lo], F32, name=f"fetched{lo}")
+        gated = {lo: keep.tile([P, 2, hi - lo], F32, name=f"gated{lo}") for lo, hi in BOTH}
 
-        def product(c, lo, hi):
-            nc.vector.tensor_tensor(
-                z[c][:, lo:hi],
-                y[:].indirect(pos_t[c][:, lo // 16 : hi // 16]),
-                gate_t[:, c, lo:hi],
-                MULT,
-            )
+        def results(c, lo, hi):
+            return y[:].indirect(pos_t[c][:, lo // 16 : hi // 16])
 
-        def add_on_tensor(lo, hi):
-            turned = psum.tile([P, hi - lo], F32, name=f"turned{lo}")
-            for t in range(lo, hi, P):
-                for c in range(2):
-                    nc.tensor.matmul(
-                        turned[:, t - lo : t - lo + P],
-                        z[c][:, t : t + P],
-                        ident[:],
-                        start=(c == 0),
-                        stop=(c == 1),
-                        is_transpose=True,
-                    )
-            total = keep.tile([P, hi - lo], F32, name=f"total{lo}")
-            nc.scalar.copy(total[:], turned[:])
-            back = psum.tile([P, hi - lo], F32, name=f"back{lo}")
-            for t in range(0, hi - lo, P):
-                nc.tensor.transpose(back[:, t : t + P], total[:, t : t + P], ident[:])
-            nc.scalar.copy(o[:, lo:hi], back[:])
-            nc.scalar.dma_start(out[:, lo:hi], o[:, lo:hi])
-
-        def add_on_vector(lo, hi):
-            nc.vector.tensor_tensor(o[:, lo:hi], z[0][:, lo:hi], z[1][:, lo:hi], ADD)
+        def store(lo, hi, one, other):
+            nc.vector.tensor_tensor(o[:, lo:hi], one, other, ADD)
             nc.sync.dma_start(out[:, lo:hi], o[:, lo:hi])
 
-        for lo, hi in ((0, 384), (384, SPLIT)):
-            product(0, lo, hi)
-            product(1, lo, hi)
-            add_on_tensor(lo, hi)
-        product(0, SPLIT, 960)
-        product(1, SPLIT, 960)
-        product(0, 960, TOKENS)
-        add_on_vector(SPLIT, 960)
-        product(1, 960, 1152)
-        product(1, 1152, TOKENS)
-        add_on_vector(960, 1152)
-        add_on_vector(1152, TOKENS)
+        for lo, hi in SECOND_ONLY:
+            nc.scalar.activation(fetched[lo][:], results(1, lo, hi), COPY)
+        for lo, hi in BOTH:
+            for c in range(2):
+                nc.scalar.activation(fetched[lo][:, c, :], results(c, lo, hi), COPY)
+
+        nc.vector.tensor_tensor(first[:], results(0, 0, SHARED), gate_t[:, 0, 0:SHARED], MULT)
+        for lo, hi in SECOND_ONLY:
+            nc.vector.tensor_tensor(second[:, lo:hi], fetched[lo][:], gate_t[:, 1, lo:hi], MULT)
+        behind = (0, SHARED, first[:], second[:])
+        for lo, hi in BOTH:
+            nc.vector.tensor_tensor(gated[lo][:], fetched[lo][:], gate_t[:, :, lo:hi], MULT)
+            store(*behind)
+            behind = (lo, hi, gated[lo][:, 0, :], gated[lo][:, 1, :])
+        store(*behind)

@@ -38,9 +38,9 @@ ON_GPSIMD1 = ((288, 512), (800, 1024))
 ON_VECTOR1 = (1184, 1280)
 EARLY_SLOTS = 1280
 ROW0 = (4, 0)
-SHARED = 576
-SECOND_ONLY = ((0, 288), (288, SHARED))
-BOTH = ((SHARED, 832), (832, 1024), (1024, 1152), (1152, 1280))
+SHARED = 896
+SECOND_ONLY = ((0, 448), (448, SHARED))
+BOTH = ((SHARED, 1088), (1088, 1216), (1216, 1280))
 W_LOADS = ((0, 4), (4, 8), (8, 12), (12, 16))
 GROUPS = ((0, 4), (4, 8), (8, 12), (12, 14), (14, 16))
 
@@ -237,7 +237,10 @@ def tile_moe_cap2_lin_relu2_kernel(
         nc.vector.tensor_tensor(first[:], results(0, 0, SHARED), gate_t[:, 0, 0:SHARED], MULT)
         for lo, hi in SECOND_ONLY:
             nc.vector.tensor_tensor(second[:, lo:hi], fetched[lo][:], gate_t[:, 1, lo:hi], MULT)
-        behind = (0, SHARED, first[:], second[:])
+        lo, hi = SECOND_ONLY[0]
+        store(lo, hi, first[:, lo:hi], second[:, lo:hi])
+        lo, hi = SECOND_ONLY[1]
+        behind = (lo, hi, first[:, lo:hi], second[:, lo:hi])
         for lo, hi in BOTH:
             nc.vector.tensor_tensor(gated[lo][:], fetched[lo][:], gate_t[:, :, lo:hi], MULT)
             store(*behind)

@@ -1,6 +1,7 @@
 from contextlib import ExitStack
 
 import concourse.mybir as mybir
+from concourse.masks import make_identity
 
 P = 128
 TOKENS = 1280
@@ -38,10 +39,10 @@ ON_GPSIMD1 = ((288, 512), (800, 1024))
 ON_VECTOR1 = (1184, 1280)
 EARLY_SLOTS = 1280
 ROW0 = (4, 0)
-SHARED = 896
-SECOND_ONLY = ((0, 448), (448, SHARED))
-BOTH = ((SHARED, 1088), (1088, 1216), (1216, 1280))
-W_LOADS = ((0, 4), (4, 8), (8, 12), (12, 16))
+TURNED = 256
+PIECES = ((TURNED, 576), (576, 896), (896, 1088), (1088, 1280))
+W_LOADS = ((0, 4), (4, 8), (8, 16))
+W4_LOADS = ((0, 4), (4, 8), (8, 16))
 GROUPS = ((0, 4), (4, 8), (8, 12), (12, 14), (14, 16))
 
 
@@ -60,9 +61,10 @@ def tile_moe_cap2_lin_relu2_kernel(
         offs_t = keep.tile([P, SLOTS // 16], U16, name="offs_t")
         pos_t = [keep.tile([P, TOKENS // 16], U16, name=f"pos{c}_t") for c in range(2)]
         bias_t = keep.tile([P, EXPERTS], F32, name="bias_t")
-        gate_t = keep.tile([P, 2, TOKENS], F32, name="gate_t")
+        gate_t = keep.tile([P, 2, TOKENS - TURNED], F32, name="gate_t")
+        gate_down = [keep.tile([P, TURNED // P], F32, name=f"gate_down{c}") for c in range(2)]
         w8_t = {lo: keep.tile([P, (hi - lo) * 4 * N], U8, name=f"w8_{lo}", align_bytes=64) for lo, hi in W_LOADS}
-        w4_t = {lo: keep.tile([P, (hi - lo) * 2 * N], U8, name=f"w4_{lo}", align_bytes=64) for lo, hi in W_LOADS}
+        w4_t = {lo: keep.tile([P, (hi - lo) * 2 * N], U8, name=f"w4_{lo}", align_bytes=64) for lo, hi in W4_LOADS}
         ws_t = keep.tile([P, EXPERTS * N], U8, name="ws_t", align_bytes=64)
         codes = [keep.tile([P, TOKENS], U32, name=f"codes{a}", align_bytes=64) for a in range(2)]
         scales = keep.tile([P, TOKENS], U8, name="scales", align_bytes=64)
@@ -70,6 +72,7 @@ def tile_moe_cap2_lin_relu2_kernel(
         words1 = keep.tile([P, SLOTS], U32, name="words1", align_bytes=64)
         slot_scales = keep.tile([P, SLOTS], U8, name="slot_scales", align_bytes=64)
         y = keep.tile([P, SLOTS + PAD], F32, name="y")
+        ident = keep.tile([P, P], F32, name="ident")
         grouped = [keep.tile([P, TOKENS, 4], BF16, name=f"grouped{a}", align_bytes=64) for a in range(2)]
         early0 = keep.tile([P, 2, TOKENS], F32, name="early0")
         late0 = {lo: keep.tile([P, 2, hi - lo], F32, name=f"late0_{lo}") for lo, hi in LATE_LOADS0}
@@ -77,6 +80,7 @@ def tile_moe_cap2_lin_relu2_kernel(
 
         nc.gpsimd.memset(ws_t[:].bitcast(I32), 0)
         nc.vector.memset(scales[:].bitcast(I32), 0)
+        make_identity(nc, ident[:])
         nc.vector.memset(y[:, SLOTS:], 0.0)
 
         rows = [xT[a * K_PASS : (a + 1) * K_PASS, :].rearrange("(p j) t -> p j t", j=4) for a in range(2)]
@@ -96,13 +100,20 @@ def tile_moe_cap2_lin_relu2_kernel(
         w8_src = w8_words.rearrange("e a p n r -> p (e a) (n r)").bitcast(I32)
         w4_src = w4_words.rearrange("e a p n -> p (e a) n").bitcast(I32)
         for lo, hi in W_LOADS:
-            nc.sync.dma_start(w4_t[lo][:].bitcast(I32).rearrange("p (e n) -> p e n", e=hi - lo), w4_src[:, lo:hi])
+            for lo4, hi4 in W4_LOADS:
+                if lo4 == lo:
+                    nc.sync.dma_start(
+                        w4_t[lo4][:].bitcast(I32).rearrange("p (e n) -> p e n", e=hi4 - lo4), w4_src[:, lo4:hi4]
+                    )
             nc.sync.dma_start(w8_t[lo][:].bitcast(I32).rearrange("p (e n) -> p e n", e=hi - lo), w8_src[:, lo:hi])
             if lo == 0:
                 nc.sync.dma_start(bias_t[:], b)
         nc.sync.dma_start(pos_t[0][:], pos1)
         nc.sync.dma_start(pos_t[1][:], pos2)
-        nc.sync.dma_start(gate_t[:], gate.rearrange("c n t -> n c t"))
+        with nc.allow_non_contiguous_dma(reason="one gate a partition"):
+            for c in range(2):
+                nc.sync.dma_start(gate_down[c][:], gate[c, 0, 0:TURNED].rearrange("(blk p) -> p blk", p=P))
+        nc.sync.dma_start(gate_t[:], gate[:, :, TURNED:].rearrange("c n t -> n c t"))
 
         def round_early(copy, lo, hi):
             copy(grouped[0][:, lo:hi, 0:2], early0[:, :, lo:hi].rearrange("p j t -> p t j"))
@@ -166,6 +177,7 @@ def tile_moe_cap2_lin_relu2_kernel(
                 weights = w8_t[first][:, (e - first) * 4 * N : (e - first + 1) * 4 * N].bitcast(FP8X4)
                 words = early_words[:, lo:hi] if hi <= EARLY_SLOTS else late_words[:, lo - EARLY_SLOTS : hi - EARLY_SLOTS]
             else:
+                first = start_of(W4_LOADS, e)
                 weights = w4_t[first][:, (e - first) * 2 * N : (e - first + 1) * 2 * N].bitcast(FP4X4)
                 words = words1[:, lo:hi]
             nc.tensor.matmul_mx(
@@ -214,35 +226,71 @@ def tile_moe_cap2_lin_relu2_kernel(
         activate_on_vector(EXPERTS - 1)
 
         o = keep.tile([P, TOKENS], F32, name="o")
-        first = keep.tile([P, SHARED], F32, name="first")
-        second = keep.tile([P, SHARED], F32, name="second")
-        fetched = {lo: keep.tile([P, hi - lo], F32, name=f"fetched{lo}") for lo, hi in SECOND_ONLY}
-        for lo, hi in BOTH:
-            fetched[lo] = keep.tile([P, 2, hi - lo], F32, name=f"fetched{lo}")
-        gated = {lo: keep.tile([P, 2, hi - lo], F32, name=f"gated{lo}") for lo, hi in BOTH}
+        blocks = range(TURNED // P)
 
         def results(c, lo, hi):
             return y[:].indirect(pos_t[c][:, lo // 16 : hi // 16])
 
-        def store(lo, hi, one, other):
-            nc.vector.tensor_tensor(o[:, lo:hi], one, other, ADD)
+        fetched = [keep.tile([P, TURNED], F32, name=f"fetched{c}") for c in range(2)]
+        turned = [psum.tile([P, TURNED], F32, name=f"turned{c}") for c in range(2)]
+        scaled = {(c, blk): keep.tile([P, P], F32, name=f"scaled{c}_{blk}") for c in range(2) for blk in blocks}
+        for c in range(2):
+            nc.scalar.activation(fetched[c][:], results(c, 0, TURNED), COPY)
+            for blk in blocks:
+                nc.tensor.transpose(turned[c][:, blk * P : (blk + 1) * P], fetched[c][:, blk * P : (blk + 1) * P], ident[:])
+        helped = {PIECES[1][0]: keep.tile([P, PIECES[1][1] - PIECES[1][0]], F32, name="helped")[:]}
+
+        def help_with(lo, hi):
+            nc.scalar.activation(helped[lo], results(1, lo, hi), COPY)
+
+        help_with(*PIECES[1])
+        back = psum.tile([P, TURNED], F32, name="back")
+        for blk in blocks:
+            for c in range(2):
+                nc.scalar.activation(
+                    scaled[c, blk][:], turned[c][:, blk * P : (blk + 1) * P], COPY, scale=gate_down[c][:, blk : blk + 1]
+                )
+                nc.tensor.matmul(
+                    back[:, blk * P : (blk + 1) * P],
+                    scaled[c, blk][:],
+                    ident[:],
+                    start=(c == 0),
+                    stop=(c == 1),
+                    is_transpose=True,
+                )
+        late = keep.tile([P, TOKENS - PIECES[2][0]], F32, name="fetched1")
+        for lo, hi in PIECES[2:]:
+            helped[lo] = late[:, lo - PIECES[2][0] : hi - PIECES[2][0]]
+        help_with(*PIECES[2])
+        help_with(*PIECES[3])
+        nc.scalar.copy(o[:, 0:TURNED], back[:])
+        nc.scalar.dma_start(out[:, 0:TURNED], o[:, 0:TURNED])
+
+        z = [keep.tile([P, TOKENS - TURNED], F32, name=f"z{c}") for c in range(2)]
+
+        def product(c, lo, hi, values):
+            nc.vector.tensor_tensor(z[c][:, lo - TURNED : hi - TURNED], values, gate_t[:, c, lo - TURNED : hi - TURNED], MULT)
+
+        def fetch(c, lo, hi):
+            product(c, lo, hi, results(c, lo, hi))
+
+        def take(lo, hi):
+            product(1, lo, hi, helped[lo])
+
+        def store(lo, hi):
+            mine = slice(lo - TURNED, hi - TURNED)
+            nc.vector.tensor_tensor(o[:, lo:hi], z[0][:, mine], z[1][:, mine], ADD)
             nc.sync.dma_start(out[:, lo:hi], o[:, lo:hi])
 
-        for lo, hi in SECOND_ONLY:
-            nc.scalar.activation(fetched[lo][:], results(1, lo, hi), COPY)
-        for lo, hi in BOTH:
-            for c in range(2):
-                nc.scalar.activation(fetched[lo][:, c, :], results(c, lo, hi), COPY)
-
-        nc.vector.tensor_tensor(first[:], results(0, 0, SHARED), gate_t[:, 0, 0:SHARED], MULT)
-        for lo, hi in SECOND_ONLY:
-            nc.vector.tensor_tensor(second[:, lo:hi], fetched[lo][:], gate_t[:, 1, lo:hi], MULT)
-        lo, hi = SECOND_ONLY[0]
-        store(lo, hi, first[:, lo:hi], second[:, lo:hi])
-        lo, hi = SECOND_ONLY[1]
-        behind = (lo, hi, first[:, lo:hi], second[:, lo:hi])
-        for lo, hi in BOTH:
-            nc.vector.tensor_tensor(gated[lo][:], fetched[lo][:], gate_t[:, :, lo:hi], MULT)
-            store(*behind)
-            behind = (lo, hi, gated[lo][:, 0, :], gated[lo][:, 1, :])
-        store(*behind)
+        fetch(0, *PIECES[0])
+        fetch(1, *PIECES[0])
+        fetch(0, *PIECES[1])
+        store(*PIECES[0])
+        take(*PIECES[1])
+        fetch(0, *PIECES[2])
+        store(*PIECES[1])
+        fetch(0, *PIECES[3])
+        take(*PIECES[2])
+        take(*PIECES[3])
+        store(*PIECES[2])
+        store(*PIECES[3])

@@ -190,16 +190,16 @@ def tile_moe_cap2_lin_relu2_kernel(
                 stop=(a == 1),
             )
 
-        relu = keep.tile([P, 4 * CAP], F32, name="relu")
+        relu = {lo: keep.tile([P, 2 * CAP], F32, name=f"relu{lo}") for lo in range(0, EXPERTS, 2)}
 
-        def activate_on_scalar(lo, hi):
-            for e in range(lo, hi):
-                nc.scalar.activation(relu[:, e % 4 * CAP : (e % 4 + 1) * CAP], sums[e], RELU, bias=bias_t[:, e : e + 1])
-            nc.scalar.activation(y[:, lo * CAP : hi * CAP], relu[:, lo % 4 * CAP : ((hi - 1) % 4 + 1) * CAP], SQUARE)
+        def activate_pair(lo):
+            for e in (lo, lo + 1):
+                nc.scalar.activation(relu[lo][:, e % 2 * CAP : (e % 2 + 1) * CAP], sums[e], RELU, bias=bias_t[:, e : e + 1])
+            nc.gpsimd.tensor_tensor(y[:, lo * CAP : (lo + 2) * CAP], relu[lo][:], relu[lo][:], MULT)
 
         def activate_in_halves(e):
             halves = (slice(0, CAP // 2), slice(CAP // 2, CAP))
-            mine = relu[:, e % 4 * CAP : (e % 4 + 1) * CAP]
+            mine = relu[e][:, 0:CAP]
             for half in halves:
                 nc.scalar.activation(mine[:, half], sums[e][:, half], RELU, bias=bias_t[:, e : e + 1])
             for half in halves:
@@ -211,17 +211,20 @@ def tile_moe_cap2_lin_relu2_kernel(
             for half in halves:
                 nc.vector.tensor_scalar(relu_last[:, half], sums[e][:, half], bias_t[:, e : e + 1], 0.0, ADD, MAX)
             for half in halves:
-                nc.vector.tensor_tensor(y[:, e * CAP : (e + 1) * CAP][:, half], relu_last[:, half], relu_last[:, half], MULT)
+                nc.vector.scalar_tensor_tensor(
+                    y[:, e * CAP : (e + 1) * CAP][:, half], sums[e][:, half], bias_t[:, e : e + 1], relu_last[:, half], ADD, MULT
+                )
 
         for lo, hi in GROUPS:
             gather(slot_scales[:, lo * CAP : hi * CAP], scales, lo * CAP, hi * CAP)
             for e in range(lo, hi):
                 multiply(e, 0)
             gather(words1[:, lo * CAP : hi * CAP], codes[1], lo * CAP, hi * CAP)
-            for e in range(lo, hi) if hi < EXPERTS else reversed(range(lo, hi)):
+            for e in range(lo, hi):
                 multiply(e, 1)
             if hi < EXPERTS:
-                activate_on_scalar(lo, hi)
+                for pair in range(lo, hi, 2):
+                    activate_pair(pair)
         activate_in_halves(EXPERTS - 2)
         activate_on_vector(EXPERTS - 1)
 

@@ -43,6 +43,7 @@ TURNED = 256
 PIECES = ((TURNED, 576), (576, 896), (896, 1088), (1088, 1280))
 W_LOADS = ((0, 4), (4, 8), (8, 16))
 W4_LOADS = ((0, 4), (4, 8), (8, 16))
+PAIRED = 12
 GROUPS = ((0, 4), (4, 8), (8, 12), (12, 14), (14, 16))
 
 
@@ -197,6 +198,16 @@ def tile_moe_cap2_lin_relu2_kernel(
                 nc.scalar.activation(relu[lo][:, e % 2 * CAP : (e % 2 + 1) * CAP], sums[e], RELU, bias=bias_t[:, e : e + 1])
             nc.gpsimd.tensor_tensor(y[:, lo * CAP : (lo + 2) * CAP], relu[lo][:], relu[lo][:], MULT)
 
+        def activate_one(e):
+            mine = relu[e][:, 0:CAP]
+            nc.scalar.activation(mine, sums[e], RELU, bias=bias_t[:, e : e + 1])
+            nc.gpsimd.tensor_tensor(y[:, e * CAP : (e + 1) * CAP], mine, mine, MULT)
+
+        def activate_whole_on_vector(e):
+            mine = keep.tile([P, CAP], F32, name="relu_whole")
+            nc.vector.tensor_scalar(mine[:], sums[e], bias_t[:, e : e + 1], 0.0, ADD, MAX)
+            nc.vector.scalar_tensor_tensor(y[:, e * CAP : (e + 1) * CAP], sums[e], bias_t[:, e : e + 1], mine[:], ADD, MULT)
+
         def activate_in_halves(e):
             halves = (slice(0, CAP // 2), slice(CAP // 2, CAP))
             mine = relu[e][:, 0:CAP]
@@ -222,9 +233,11 @@ def tile_moe_cap2_lin_relu2_kernel(
             gather(words1[:, lo * CAP : hi * CAP], codes[1], lo * CAP, hi * CAP)
             for e in range(lo, hi):
                 multiply(e, 1)
-            if hi < EXPERTS:
+            if hi <= PAIRED:
                 for pair in range(lo, hi, 2):
                     activate_pair(pair)
+        activate_one(PAIRED)
+        activate_whole_on_vector(PAIRED + 1)
         activate_in_halves(EXPERTS - 2)
         activate_on_vector(EXPERTS - 1)
 

@@ -44,7 +44,9 @@ PIECES = ((TURNED, 576), (576, 896), (896, 1088), (1088, 1280))
 W_LOADS = ((0, 4), (4, 8), (8, 16))
 W4_LOADS = ((0, 4), (4, 8), (8, 16))
 PAIRED = 12
-GROUPS = ((0, 4), (4, 8), (8, 12), (12, 14), (14, 16))
+GROUPS = (((0, 7), ((0, 7),)), ((7, 12), ((7, 12),)), ((12, 14), ((12, 14),)), ((14, 16), ((14, 16),)))
+BANKS = ((0, 4), (4, 7), (7, 10), (10, 12), (12, 13), (13, 14), (14, 15), (15, 16))
+SQUARES = ((0, 2), (2, 4), (4, 7), (7, 10), (10, 12))
 
 
 def start_of(ranges, col):
@@ -169,12 +171,15 @@ def tile_moe_cap2_lin_relu2_kernel(
         quantize(1, *LOADS1[2])
 
         sums = {}
+        for i, (lo, hi) in enumerate(BANKS):
+            bank = psum.tile([P, (hi - lo) * CAP], F32, name=f"bank{i}")
+            for e in range(lo, hi):
+                sums[e] = bank[:, (e - lo) * CAP : (e - lo + 1) * CAP]
 
         def multiply(e, a):
             lo, hi = e * CAP, (e + 1) * CAP
             first = start_of(W_LOADS, e)
             if a == 0:
-                sums[e] = psum.tile([P, CAP], F32, name=f"bank{e % 4}")[:]
                 weights = w8_t[first][:, (e - first) * 4 * N : (e - first + 1) * 4 * N].bitcast(FP8X4)
                 words = early_words[:, lo:hi] if hi <= EARLY_SLOTS else late_words[:, lo - EARLY_SLOTS : hi - EARLY_SLOTS]
             else:
@@ -187,21 +192,17 @@ def tile_moe_cap2_lin_relu2_kernel(
                 lhsT_scale=ws_t[ROW0[a] :, e * N : (e + 1) * N],
                 rhs=words.bitcast(FP8X4),
                 rhs_scale=slot_scales[ROW0[a] :, lo:hi],
-                start=(a == 0),
-                stop=(a == 1),
+                start=(a == 0 and any(e == first for first, last in BANKS)),
+                stop=(a == 1 and any(e + 1 == last for first, last in BANKS)),
             )
 
-        relu = {lo: keep.tile([P, 2 * CAP], F32, name=f"relu{lo}") for lo in range(0, EXPERTS, 2)}
+        relu = keep.tile([P, SLOTS], F32, name="relu")
 
-        def activate_pair(lo):
-            for e in (lo, lo + 1):
-                nc.scalar.activation(relu[lo][:, e % 2 * CAP : (e % 2 + 1) * CAP], sums[e], RELU, bias=bias_t[:, e : e + 1])
-            nc.gpsimd.tensor_tensor(y[:, lo * CAP : (lo + 2) * CAP], relu[lo][:], relu[lo][:], MULT)
-
-        def activate_one(e):
-            mine = relu[e][:, 0:CAP]
-            nc.scalar.activation(mine, sums[e], RELU, bias=bias_t[:, e : e + 1])
-            nc.gpsimd.tensor_tensor(y[:, e * CAP : (e + 1) * CAP], mine, mine, MULT)
+        def activate_with_gpsimd(lo, hi):
+            for e in range(lo, hi):
+                nc.scalar.activation(relu[:, e * CAP : (e + 1) * CAP], sums[e], RELU, bias=bias_t[:, e : e + 1])
+            mine = slice(lo * CAP, hi * CAP)
+            nc.gpsimd.tensor_tensor(y[:, mine], relu[:, mine], relu[:, mine], MULT)
 
         def activate_whole_on_vector(e):
             mine = keep.tile([P, CAP], F32, name="relu_whole")
@@ -210,7 +211,7 @@ def tile_moe_cap2_lin_relu2_kernel(
 
         def activate_in_halves(e):
             halves = (slice(0, CAP // 2), slice(CAP // 2, CAP))
-            mine = relu[e][:, 0:CAP]
+            mine = relu[:, e * CAP : (e + 1) * CAP]
             for half in halves:
                 nc.scalar.activation(mine[:, half], sums[e][:, half], RELU, bias=bias_t[:, e : e + 1])
             for half in halves:
@@ -226,17 +227,18 @@ def tile_moe_cap2_lin_relu2_kernel(
                     y[:, e * CAP : (e + 1) * CAP][:, half], sums[e][:, half], bias_t[:, e : e + 1], relu_last[:, half], ADD, MULT
                 )
 
-        for lo, hi in GROUPS:
+        for (lo, hi), parts in GROUPS:
             gather(slot_scales[:, lo * CAP : hi * CAP], scales, lo * CAP, hi * CAP)
             for e in range(lo, hi):
                 multiply(e, 0)
-            gather(words1[:, lo * CAP : hi * CAP], codes[1], lo * CAP, hi * CAP)
-            for e in range(lo, hi):
-                multiply(e, 1)
-            if hi <= PAIRED:
-                for pair in range(lo, hi, 2):
-                    activate_pair(pair)
-        activate_one(PAIRED)
+            for first, last in parts:
+                gather(words1[:, first * CAP : last * CAP], codes[1], first * CAP, last * CAP)
+                for e in range(first, last):
+                    multiply(e, 1)
+                for square in SQUARES:
+                    if first <= square[0] < last:
+                        activate_with_gpsimd(*square)
+        activate_with_gpsimd(PAIRED, PAIRED + 1)
         activate_whole_on_vector(PAIRED + 1)
         activate_in_halves(EXPERTS - 2)
         activate_on_vector(EXPERTS - 1)
@@ -248,7 +250,7 @@ def tile_moe_cap2_lin_relu2_kernel(
             return y[:].indirect(pos_t[c][:, lo // 16 : hi // 16])
 
         fetched = [keep.tile([P, TURNED], F32, name=f"fetched{c}") for c in range(2)]
-        turned = [psum.tile([P, TURNED], F32, name=f"turned{c}") for c in range(2)]
+        turned = [psum.tile([P, TURNED], F32, name=f"bank{c}") for c in range(2)]
         scaled = {(c, blk): keep.tile([P, P], F32, name=f"scaled{c}_{blk}") for c in range(2) for blk in blocks}
         for c in range(2):
             nc.scalar.activation(fetched[c][:], results(c, 0, TURNED), COPY)
@@ -260,7 +262,7 @@ def tile_moe_cap2_lin_relu2_kernel(
             nc.scalar.activation(helped[lo], results(1, lo, hi), COPY)
 
         help_with(*PIECES[1])
-        back = psum.tile([P, TURNED], F32, name="back")
+        back = psum.tile([P, TURNED], F32, name="bank2")
         for blk in blocks:
             for c in range(2):
                 nc.scalar.activation(

@@ -45,8 +45,8 @@ W_LOADS = ((0, 4), (4, 8), (8, 16))
 W4_LOADS = ((0, 4), (4, 8), (8, 16))
 PAIRED = 12
 GROUPS = (((0, 7), ((0, 7),)), ((7, 12), ((7, 12),)), ((12, 14), ((12, 14),)), ((14, 16), ((14, 16),)))
-BANKS = ((0, 4), (4, 7), (7, 10), (10, 12), (12, 13), (13, 14), (14, 15), (15, 16))
-SQUARES = ((0, 2), (2, 4), (4, 7), (7, 10), (10, 12))
+BANKS = ((0, 4), (4, 7), (7, 9), (9, 12), (12, 13), (13, 14), (14, 15), (15, 16))
+SQUARES = ((0, 2), (2, 4), (4, 7), (7, 9), (9, 12))
 
 
 def start_of(ranges, col):
@@ -238,7 +238,9 @@ def tile_moe_cap2_lin_relu2_kernel(
                 for square in SQUARES:
                     if first <= square[0] < last:
                         activate_with_gpsimd(*square)
-        activate_with_gpsimd(PAIRED, PAIRED + 1)
+        mine = slice(PAIRED * CAP, (PAIRED + 1) * CAP)
+        nc.scalar.activation(relu[:, mine], sums[PAIRED], RELU, bias=bias_t[:, PAIRED : PAIRED + 1])
+        nc.scalar.activation(y[:, mine], relu[:, mine], SQUARE)
         activate_whole_on_vector(PAIRED + 1)
         activate_in_halves(EXPERTS - 2)
         activate_on_vector(EXPERTS - 1)

from contextlib import ExitStack

import concourse.mybir as mybir
from concourse.masks import make_identity

P = 128
TOKENS = 1280
EXPERTS = 16
CAP = 128
SLOTS = EXPERTS * CAP
N = 128
PAD = 32
K_PASS = 512
FLOPS = 2 * SLOTS * 2 * K_PASS * N

F32 = mybir.dt.float32
BF16 = mybir.dt.bfloat16
U32 = mybir.dt.uint32
I32 = mybir.dt.int32
U16 = mybir.dt.uint16
U8 = mybir.dt.uint8
FP8X4 = mybir.dt.float8_e4m3fn_x4
FP4X4 = mybir.dt.float4_e2m1fn_x4
MULT = mybir.AluOpType.mult
ADD = mybir.AluOpType.add
MAX = mybir.AluOpType.max
RELU = mybir.ActivationFunctionType.Relu
SQUARE = mybir.ActivationFunctionType.Square
COPY = mybir.ActivationFunctionType.Copy

LATE_LOADS0 = ((0, 768), (768, 1280))
EARLY_ON_VECTOR0 = 832
LATE_ON_VECTOR0 = ((0, 256), (256, 384), (768, 1024))
LATE_ON_SCALAR0 = ((384, 512), (512, 768), (1024, 1280))
UNITS0 = ((0, 256), (256, 512), (512, 768), (768, 1024), (1024, 1280))
LOADS1 = ((0, 512), (512, 1024), (1024, 1280))
ON_SCALAR1 = ((0, 288), (512, 800), (1024, 1184))
ON_GPSIMD1 = ((288, 512), (800, 1024))
ON_VECTOR1 = (1184, 1280)
EARLY_SLOTS = 1280
ROW0 = (4, 0)
TURNED = 256
PIECES = ((TURNED, 576), (576, 896), (896, 1088), (1088, 1280))
W_LOADS = ((0, 4), (4, 8), (8, 16))
W4_LOADS = ((0, 4), (4, 8), (8, 16))
PAIRED = 12
GROUPS = (((0, 7), ((0, 7),)), ((7, 12), ((7, 12),)), ((12, 14), ((12, 14),)), ((14, 16), ((14, 16),)))
BANKS = ((0, 4), (4, 7), (7, 9), (9, 12), (12, 13), (13, 14), (14, 15), (15, 16))
SQUARES = ((0, 2), (2, 4), (4, 7), (7, 9), (9, 12))


def start_of(ranges, col):
    return max(lo for lo, hi in ranges if lo <= col)


def tile_moe_cap2_lin_relu2_kernel(
    tc, xT, w8_words, w8_scales, w4_words, w4_scales, b, gate, offs, pos1, pos2, out
):
    nc = tc.nc
    with ExitStack() as ctx:
        keep = ctx.enter_context(tc.tile_pool(name="keep", bufs=1))
        psum = ctx.enter_context(tc.psum_pool(name="psum", bufs=1))

        offs_t = keep.tile([P, SLOTS // 16], U16, name="offs_t")
        pos_t = [keep.tile([P, TOKENS // 16], U16, name=f"pos{c}_t") for c in range(2)]
        bias_t = keep.tile([P, EXPERTS], F32, name="bias_t")
        gate_t = keep.tile([P, 2, TOKENS - TURNED], F32, name="gate_t")
        gate_down = [keep.tile([P, TURNED // P], F32, name=f"gate_down{c}") for c in range(2)]
        w8_t = {lo: keep.tile([P, (hi - lo) * 4 * N], U8, name=f"w8_{lo}", align_bytes=64) for lo, hi in W_LOADS}
        w4_t = {lo: keep.tile([P, (hi - lo) * 2 * N], U8, name=f"w4_{lo}", align_bytes=64) for lo, hi in W4_LOADS}
        ws_t = keep.tile([P, EXPERTS * N], U8, name="ws_t", align_bytes=64)
        codes = [keep.tile([P, TOKENS], U32, name=f"codes{a}", align_bytes=64) for a in range(2)]
        scales = keep.tile([P, TOKENS], U8, name="scales", align_bytes=64)
        early_words = keep.tile([P, EARLY_SLOTS], U32, name="early_words", align_bytes=64)
        words1 = keep.tile([P, SLOTS], U32, name="words1", align_bytes=64)
        slot_scales = keep.tile([P, SLOTS], U8, name="slot_scales", align_bytes=64)
        y = keep.tile([P, SLOTS + PAD], F32, name="y")
        ident = keep.tile([P, P], F32, name="ident")
        grouped = [keep.tile([P, TOKENS, 4], BF16, name=f"grouped{a}", align_bytes=64) for a in range(2)]
        early0 = keep.tile([P, 2, TOKENS], F32, name="early0")
        late0 = {lo: keep.tile([P, 2, hi - lo], F32, name=f"late0_{lo}") for lo, hi in LATE_LOADS0}
        raw1 = {lo: keep.tile([P, 4, hi - lo], F32, name=f"raw1_{lo}", align_bytes=64) for lo, hi in LOADS1}

        nc.gpsimd.memset(ws_t[:].bitcast(I32), 0)
        nc.vector.memset(scales[:].bitcast(I32), 0)
        make_identity(nc, ident[:])
        nc.vector.memset(y[:, SLOTS:], 0.0)

        rows = [xT[a * K_PASS : (a + 1) * K_PASS, :].rearrange("(p j) t -> p j t", j=4) for a in range(2)]
        nc.sync.dma_start(early0[:], rows[0][:, 0:2, :])
        for lo, hi in LATE_LOADS0:
            nc.sync.dma_start(late0[lo][:], rows[0][:, 2:4, lo:hi])
        nc.sync.dma_start(offs_t[:], offs)
        for lo, hi in LOADS1:
            nc.sync.dma_start(raw1[lo][:], rows[1][:, :, lo:hi])
        ws_i32 = ws_t[:].bitcast(I32).rearrange("p (e n) -> p e n", e=EXPERTS)
        for row0, src in zip(ROW0, (w8_scales, w4_scales)):
            scale_rows = src.rearrange("e a q n -> q (e a) n").bitcast(I32)
            for quad in range(4):
                nc.sync.dma_start(
                    ws_i32[32 * quad + row0 : 32 * quad + row0 + 4], scale_rows[4 * quad : 4 * quad + 4]
                )
        w8_src = w8_words.rearrange("e a p n r -> p (e a) (n r)").bitcast(I32)
        w4_src = w4_words.rearrange("e a p n -> p (e a) n").bitcast(I32)
        for lo, hi in W_LOADS:
            for lo4, hi4 in W4_LOADS:
                if lo4 == lo:
                    nc.sync.dma_start(
                        w4_t[lo4][:].bitcast(I32).rearrange("p (e n) -> p e n", e=hi4 - lo4), w4_src[:, lo4:hi4]
                    )
            nc.sync.dma_start(w8_t[lo][:].bitcast(I32).rearrange("p (e n) -> p e n", e=hi - lo), w8_src[:, lo:hi])
            if lo == 0:
                nc.sync.dma_start(bias_t[:], b)
        nc.sync.dma_start(pos_t[0][:], pos1)
        nc.sync.dma_start(pos_t[1][:], pos2)
        with nc.allow_non_contiguous_dma(reason="one gate a partition"):
            for c in range(2):
                nc.sync.dma_start(gate_down[c][:], gate[c, 0, 0:TURNED].rearrange("(blk p) -> p blk", p=P))
        nc.sync.dma_start(gate_t[:], gate[:, :, TURNED:].rearrange("c n t -> n c t"))

        def round_early(copy, lo, hi):
            copy(grouped[0][:, lo:hi, 0:2], early0[:, :, lo:hi].rearrange("p j t -> p t j"))

        def round_late(copy, lo, hi):
            first = start_of(LATE_LOADS0, lo)
            copy(grouped[0][:, lo:hi, 2:4], late0[first][:, :, lo - first : hi - first].rearrange("p j t -> p t j"))

        def round_by_fours(copy, lo, hi):
            first = start_of(LOADS1, lo)
            copy(
                grouped[1][:, lo:hi, :].rearrange("p (c i) j -> p c j i", i=4),
                raw1[first][:, :, lo - first : hi - first].rearrange("p j (c i) -> p c j i", i=4),
            )

        def round_by_token(lo, hi):
            first = start_of(LOADS1, lo)
            nc.gpsimd.tensor_copy(
                grouped[1][:, lo:hi, :], raw1[first][:, :, lo - first : hi - first].rearrange("p j t -> p t j")
            )

        def quantize(a, lo, hi):
            nc.vector.quantize_mx(
                out=codes[a][:, lo:hi].bitcast(FP8X4),
                scales=scales[ROW0[a] :, lo:hi],
                in_=grouped[a][:, lo:hi, :].rearrange("p t j -> p (t j)"),
            )

        def gather(dst, window, lo, hi):
            nc.vector.tensor_copy(dst, window[:].indirect(offs_t[:, lo // 16 : hi // 16]))

        round_early(nc.vector.tensor_copy, 0, EARLY_ON_VECTOR0)
        round_early(nc.scalar.copy, EARLY_ON_VECTOR0, TOKENS)
        for lo, hi in LATE_ON_SCALAR0:
            round_late(nc.scalar.copy, lo, hi)
        for lo, hi in LATE_ON_VECTOR0:
            round_late(nc.vector.tensor_copy, lo, hi)
        for lo, hi in UNITS0:
            quantize(0, lo, hi)

        for lo, hi in ON_SCALAR1:
            round_by_fours(nc.scalar.copy, lo, hi)
        for lo, hi in ON_GPSIMD1:
            round_by_token(lo, hi)
        for lo in (0, EARLY_SLOTS // 2):
            gather(early_words[:, lo : lo + EARLY_SLOTS // 2], codes[0], lo, lo + EARLY_SLOTS // 2)
        quantize(1, *LOADS1[0])
        late_words = keep.tile([P, SLOTS - EARLY_SLOTS], U32, name="raw1_0", align_bytes=64)
        gather(late_words[:], codes[0], EARLY_SLOTS, SLOTS)
        round_by_fours(nc.vector.tensor_copy, *ON_VECTOR1)
        quantize(1, *LOADS1[1])
        quantize(1, *LOADS1[2])

        sums = {}
        for i, (lo, hi) in enumerate(BANKS):
            bank = psum.tile([P, (hi - lo) * CAP], F32, name=f"bank{i}")
            for e in range(lo, hi):
                sums[e] = bank[:, (e - lo) * CAP : (e - lo + 1) * CAP]

        def multiply(e, a):
            lo, hi = e * CAP, (e + 1) * CAP
            first = start_of(W_LOADS, e)
            if a == 0:
                weights = w8_t[first][:, (e - first) * 4 * N : (e - first + 1) * 4 * N].bitcast(FP8X4)
                words = early_words[:, lo:hi] if hi <= EARLY_SLOTS else late_words[:, lo - EARLY_SLOTS : hi - EARLY_SLOTS]
            else:
                first = start_of(W4_LOADS, e)
                weights = w4_t[first][:, (e - first) * 2 * N : (e - first + 1) * 2 * N].bitcast(FP4X4)
                words = words1[:, lo:hi]
            nc.tensor.matmul_mx(
                out=sums[e],
                lhsT=weights,
                lhsT_scale=ws_t[ROW0[a] :, e * N : (e + 1) * N],
                rhs=words.bitcast(FP8X4),
                rhs_scale=slot_scales[ROW0[a] :, lo:hi],
                start=(a == 0 and any(e == first for first, last in BANKS)),
                stop=(a == 1 and any(e + 1 == last for first, last in BANKS)),
            )

        relu = keep.tile([P, SLOTS], F32, name="relu")

        def activate_with_gpsimd(lo, hi):
            for e in range(lo, hi):
                nc.scalar.activation(relu[:, e * CAP : (e + 1) * CAP], sums[e], RELU, bias=bias_t[:, e : e + 1])
            mine = slice(lo * CAP, hi * CAP)
            nc.gpsimd.tensor_tensor(y[:, mine], relu[:, mine], relu[:, mine], MULT)

        def activate_whole_on_vector(e):
            mine = keep.tile([P, CAP], F32, name="relu_whole")
            nc.vector.tensor_scalar(mine[:], sums[e], bias_t[:, e : e + 1], 0.0, ADD, MAX)
            nc.vector.scalar_tensor_tensor(y[:, e * CAP : (e + 1) * CAP], sums[e], bias_t[:, e : e + 1], mine[:], ADD, MULT)

        def activate_in_halves(e):
            halves = (slice(0, CAP // 2), slice(CAP // 2, CAP))
            mine = relu[:, e * CAP : (e + 1) * CAP]
            for half in halves:
                nc.scalar.activation(mine[:, half], sums[e][:, half], RELU, bias=bias_t[:, e : e + 1])
            for half in halves:
                nc.scalar.activation(y[:, e * CAP : (e + 1) * CAP][:, half], mine[:, half], SQUARE)

        def activate_on_vector(e):
            relu_last = keep.tile([P, CAP], F32, name="relu_last")
            halves = (slice(0, CAP // 2), slice(CAP // 2, CAP))
            for half in halves:
                nc.vector.tensor_scalar(relu_last[:, half], sums[e][:, half], bias_t[:, e : e + 1], 0.0, ADD, MAX)
            for half in halves:
                nc.vector.scalar_tensor_tensor(
                    y[:, e * CAP : (e + 1) * CAP][:, half], sums[e][:, half], bias_t[:, e : e + 1], relu_last[:, half], ADD, MULT
                )

        for (lo, hi), parts in GROUPS:
            gather(slot_scales[:, lo * CAP : hi * CAP], scales, lo * CAP, hi * CAP)
            for e in range(lo, hi):
                multiply(e, 0)
            for first, last in parts:
                gather(words1[:, first * CAP : last * CAP], codes[1], first * CAP, last * CAP)
                for e in range(first, last):
                    multiply(e, 1)
                for square in SQUARES:
                    if first <= square[0] < last:
                        activate_with_gpsimd(*square)
        mine = slice(PAIRED * CAP, (PAIRED + 1) * CAP)
        nc.scalar.activation(relu[:, mine], sums[PAIRED], RELU, bias=bias_t[:, PAIRED : PAIRED + 1])
        nc.scalar.activation(y[:, mine], relu[:, mine], SQUARE)
        activate_whole_on_vector(PAIRED + 1)
        activate_in_halves(EXPERTS - 2)
        activate_on_vector(EXPERTS - 1)

        o = keep.tile([P, TOKENS], F32, name="o")
        blocks = range(TURNED // P)

        def results(c, lo, hi):
            return y[:].indirect(pos_t[c][:, lo // 16 : hi // 16])

        fetched = [keep.tile([P, TURNED], F32, name=f"fetched{c}") for c in range(2)]
        turned = [psum.tile([P, TURNED], F32, name=f"bank{c}") for c in range(2)]
        scaled = {(c, blk): keep.tile([P, P], F32, name=f"scaled{c}_{blk}") for c in range(2) for blk in blocks}
        for c in range(2):
            nc.scalar.activation(fetched[c][:], results(c, 0, TURNED), COPY)
            for blk in blocks:
                nc.tensor.transpose(turned[c][:, blk * P : (blk + 1) * P], fetched[c][:, blk * P : (blk + 1) * P], ident[:])
        helped = {PIECES[1][0]: keep.tile([P, PIECES[1][1] - PIECES[1][0]], F32, name="helped")[:]}

        def help_with(lo, hi):
            nc.scalar.activation(helped[lo], results(1, lo, hi), COPY)

        help_with(*PIECES[1])
        back = psum.tile([P, TURNED], F32, name="bank2")
        for blk in blocks:
            for c in range(2):
                nc.scalar.activation(
                    scaled[c, blk][:], turned[c][:, blk * P : (blk + 1) * P], COPY, scale=gate_down[c][:, blk : blk + 1]
                )
                nc.tensor.matmul(
                    back[:, blk * P : (blk + 1) * P],
                    scaled[c, blk][:],
                    ident[:],
                    start=(c == 0),
                    stop=(c == 1),
                    is_transpose=True,
                )
        late = keep.tile([P, TOKENS - PIECES[2][0]], F32, name="fetched1")
        for lo, hi in PIECES[2:]:
            helped[lo] = late[:, lo - PIECES[2][0] : hi - PIECES[2][0]]
        help_with(*PIECES[2])
        help_with(*PIECES[3])
        nc.scalar.copy(o[:, 0:TURNED], back[:])
        nc.scalar.dma_start(out[:, 0:TURNED], o[:, 0:TURNED])

        z = [keep.tile([P, TOKENS - TURNED], F32, name=f"z{c}") for c in range(2)]

        def product(c, lo, hi, values):
            nc.vector.tensor_tensor(z[c][:, lo - TURNED : hi - TURNED], values, gate_t[:, c, lo - TURNED : hi - TURNED], MULT)

        def fetch(c, lo, hi):
            product(c, lo, hi, results(c, lo, hi))

        def take(lo, hi):
            product(1, lo, hi, helped[lo])

        def store(lo, hi):
            mine = slice(lo - TURNED, hi - TURNED)
            nc.vector.tensor_tensor(o[:, lo:hi], z[0][:, mine], z[1][:, mine], ADD)
            nc.sync.dma_start(out[:, lo:hi], o[:, lo:hi])

        fetch(0, *PIECES[0])
        fetch(1, *PIECES[0])
        fetch(0, *PIECES[1])
        store(*PIECES[0])
        take(*PIECES[1])
        fetch(0, *PIECES[2])
        store(*PIECES[1])
        fetch(0, *PIECES[3])
        take(*PIECES[2])
        take(*PIECES[3])
        store(*PIECES[2])
        store(*PIECES[3])
